import numpy as np, ml_dtypes
CORES = [3,11,19,27,35,43,51,59]
N = 8
import mx_ref
BF = ml_dtypes.bfloat16
def gcols(t, e):
    v = np.concatenate([t.reshape(8, 16, -1, 4), np.zeros((8, 16, 1, 4), BF)], axis=2)
    return np.ascontiguousarray(np.stack([v[g][:, e[g]] for g in range(8)])).reshape(128, -1)
def tile(rs):
    return np.stack(rs, axis=2).reshape(128, -1).astype(BF)
def cut(t, i, w=512):
    return t[:, w * i:w * i + w]
def pick(q, e):
    c = np.concatenate([q[0].reshape(128, -1, 4), np.zeros((128, 1, 4), np.uint8)], axis=1); s = np.concatenate([q[1], np.ones((16, 1), np.uint8)], axis=1)
    return (np.ascontiguousarray(c[:, e].reshape(128, -1)), np.ascontiguousarray(s[:, e]))
def join(*qs):
    return (np.concatenate([q[0] for q in qs], axis=1), np.concatenate([q[1] for q in qs], axis=1))
def put(q, e, v):
    c, s = q[0].reshape(128, -1, 4).copy(), q[1].copy(); c[:, e] = v[0].reshape(128, -1, 4); s[:, e] = v[1]
    return (c.reshape(128, -1), s)
def pk(c, s):
    return (np.ascontiguousarray(c), mx_ref.live(s))
def emit(q):
    return q[0], q[1]
def packed(v, rng):
    q = [mx_ref.quantize(np.ascontiguousarray(v[r])) for r in range(N)]
    return np.stack([a for a, b in q]), np.stack([mx_ref.plane(b, rng) for a, b in q])
def values_of_codes():
    e, c = np.zeros((128, 128, 4), np.float32), np.zeros((128, 2, 4), np.uint8)
    e[np.arange(128), np.arange(128), 0] = 1
    c[:127, :, 0] = np.arange(256).reshape(2, 128).T[:127]
    return mx_ref.matmul(mx_ref.quantize(e.reshape(128, 512).astype(BF)), (c.reshape(128, 8), np.full((16, 2), 127, np.uint8))).T.reshape(-1).astype(np.float64)
CODE_VALUE, SCALE_VALUE = values_of_codes(), 2.0 ** (np.arange(256) - 127.0)
def decode(q):
    return (CODE_VALUE[q[0]].reshape(16, 8, -1, 4) * SCALE_VALUE[q[1]][:, None, :, None] + 0.0).reshape(128, -1).astype(np.float32)
def f(rng, *shape):
    return mx_ref.flush((rng.standard_normal(shape, dtype=np.float32) * np.exp2(rng.integers(-2, 3, shape[:-1] + (1,)))).astype(BF))
def wide(rng, *shape, cols=0):
    v = rng.standard_normal(shape, dtype=np.float32) * np.exp2(rng.integers(-12, 13, shape)).astype(np.float32)
    if cols: v *= np.repeat(np.exp2(rng.integers(-cols, cols + 1, shape[:-2] + (1, shape[-1] // 4))) * (rng.random(shape[:-2] + (1, shape[-1] // 4)) > 0.0625), 4, axis=-1).astype(np.float32)
    return mx_ref.flush(v.astype(BF))
C, K, M, S, H, R = 384, 192, 64, 6, 8, 3
STEP = [1, 3, 5]
def gap(p, q):
    return np.abs(p.reshape(8, M, 1, S) - q.reshape(8, 1, M, S))
def match(p, q, lag):
    back = (np.arange(C) - lag[:, None]) % C
    d = np.maximum(gap(p, q), gap(np.take_along_axis(p, back, 1), np.take_along_axis(q, back, 1)))
    m = (S * np.argmin(d, axis=2) + np.arange(S)).reshape(8, C)
    e = np.sort(np.argsort(np.min(d, axis=2).reshape(8, C), axis=1, kind="stable")[:, :K], axis=1)
    return e, np.take_along_axis(m, e, 1)
def gput(t, e, h):
    a, b = t.reshape(8, 16, -1, 4).copy(), h.reshape(8, 16, -1, 4)
    for g in range(8): a[g][:, e[g]] = b[g]
    return a.reshape(128, -1)
def big(v):
    v = v.astype(np.float32)
    v[np.abs(v) < np.float32(2.0 ** -16)] = 0
    return v.astype(BF)
def numbers_of(rng):
    return {"x": big(f(rng, N, 128, 4 * C)), "u": np.array(f(rng, N, 128, 512)), "v": np.array(f(rng, N, 128, 512))}
def weights(rng, still=[]):
    w = big(f(rng, N, 128, 2048)).reshape(N, 8, 16, 4, 8, 16, 4)
    for i in still:
        w[:, :, i] = 0
        w[:, :, :, :, :, i] = 0
    c, p = packed(w.reshape(N, 128, 2048), rng)
    return {"wc": c, "ws": p}
def setup_inputs(rng):
    return {**numbers_of(rng), **weights(rng)}
def setup_inputs_ties(rng):
    d = numbers_of(rng)
    e = rng.permutation(N)
    x = d["x"].reshape(N, 8, 16, C, 4)
    a = x[0][:, :8, :3].copy()
    a[:, :, 2] = 0
    for r in range(N):
        k = np.zeros(C, int) if r == e[0] else rng.permutation(C) % 3
        x[r][:, :8] = a[:, :, k]
    x[e[1]] = 0
    u = d["u"].reshape(N, 8, 16, 128, 4)
    u[1:, :, :, ::32] = u[:1, :, :, ::32].copy()
    u[:, :, 8:, ::16] = 0
    return {"x": x.reshape(N, 128, 4 * C), "u": u.reshape(N, 128, 512), "v": d["v"], **weights(rng, range(8))}
def setup_inputs_near(rng):
    d = numbers_of(rng)
    x = d["x"].astype(np.float32).reshape(N, 8, 16, C, 4)
    u = d["u"].reshape(N, 128, 128, 4)
    u[:, :, ::16] = 0
    x[:, :, 0] = 0
    o = rng.permutation(8) % 4
    for r in range(N):
        for g in range(8):
            size = 2.0 ** -7 if o[g] == 3 else 1.0
            sign = -1.0 if r % 2 == 1 and o[g] < 3 else 1.0
            s = rng.integers(0, 256, C)
            b = ((s[:, None] >> np.arange(8)) & 1) * np.exp2(np.arange(8) - 23.0) * size * sign
            x[r, g, 8] = b[:, :4]
            x[r, g, 9] = b[:, 4:]
            x[r, g, 10:] = rng.integers(4, 8, (6, C, 4)) * 2.0 ** -20 * size
            if sign < 0: x[r, g, 0, :, 0] = -1
            if o[g] % 2 == 0 or o[g] == 3 and r % 2 == 0: x[r, g, 0, int(rng.integers(C)), 0] = sign * 2.0 ** 30
            k = 2.0 ** -30 if o[g] >= 2 else 1.0
            u[r, 16 * g, 16 * g, 0] = 1.0 if o[g] == 3 else k
            u[r, 16 * g + 8:16 * g + 10, 16 * g] = k
            if sign < 0 and r % 4 == 1:
                x[r, g, 0, :, 1] = -2.0 ** -9
                u[r, 16 * g, 16 * g, 1] = k
            if o[g] == 3:
                h = rng.integers(0, 6, C)
                x[r, g, 10, :, 0] = (8 + h) * 2.0 ** -33
                x[r, g, 11, :, 0] = (9 + h) * 2.0 ** -33
                u[r, 16 * g + 10, 16 * g, 0] = 9 * 2.0 ** -33
                u[r, 16 * g + 11, 16 * g, 0] = -8 * 2.0 ** -33
    return {"x": x.reshape(N, 128, 4 * C).astype(BF), "u": u.reshape(N, 128, 512), "v": d["v"], **weights(rng, [0, 8, 9, 10, 11, 12, 13, 14, 15])}
def setup_inputs_lags(rng):
    d = numbers_of(rng)
    x = d["x"].astype(np.float32).reshape(N, 8, 16, C, 4)
    u = d["u"].reshape(N, 128, 128, 4)
    size = np.where(rng.permutation(N) < N // 2, 2.0 ** -30, 1.0).astype(np.float32)
    x[:, :, :11] = 0
    ring = np.argsort(rng.random((8, C)), axis=1)
    key = np.zeros((N, 8, C), int)
    full, first = rng.permutation(8) < 4, rng.integers(0, S, 8)
    kept = [0, 1, 3, 4] if S == 8 else [0, 1, 3]
    for r in range(N):
        n = rng.permutation([0, 1, 2, 3, C // 2 + 2, 257, C - 1, C])
        for g in range(8):
            a = np.where(rng.permutation(C) < n[g], 1, -rng.integers(0, 2, C)) * size[r]
            x[r, g, 0, :, 0] = a * 1.125
            x[r, g, 1, :, 0] = a * 1.25
            gone, new = rng.permutation(C) < C // 4, rng.permutation(C)
            if full[g]: gone, new = ~np.isin((np.arange(C) - first[g]) % S, kept), new + 512 * (r % 2)
            key[r, g] = np.where(gone, new, np.roll(ring[g], S * int(rng.integers(M))))
    z = ((key[:, :, :, None] >> np.arange(12)) & 1) * np.exp2(np.arange(12.0))
    for i in range(3): x[:, :, 8 + i] = z[:, :, :, 4 * i:4 * i + 4]
    u[:, :, ::16] = 0
    u[:, :, 1::16] = 0
    for h in range(0, 128, 16):
        u[:, h + 8:h + 11, h] = 1
        u[:, h, h + 1, 0] = (size * np.float32(1.125)).astype(BF)
        u[:, h + 1, h + 1, 0] = (-size).astype(BF)
    return {"x": x.reshape(N, 128, 4 * C).astype(BF), "u": u.reshape(N, 128, 512), "v": d["v"], **weights(rng, range(11))}
def setup_inputs_huge(rng):
    d = numbers_of(rng)
    x = 2.0 ** 30 * (0.9 + 0.1 * rng.random((N, 128, C, 4)))
    x[:, ::8] = 2.0 ** 30
    far, c = rng.permutation(8) % 2, rng.permutation(8) % 2 * 2.0 - 1.0
    u = d["u"].reshape(N, 128, 8, 16, 4)
    for r in range(N):
        k = np.where((far == 1) & (r % 2 == 1), -c, c)
        a = 2.0 ** 30 * (1 - 0.05 * rng.random((128, 8, 4)))
        a[::8] = 2.0 ** 30
        u[r, :, :, 0] = (a * k[:, None]).astype(np.float32).astype(BF)
    w = np.zeros((N, 128, 4, 128, 4), np.float32)
    i = np.flatnonzero(np.arange(128) % 8)
    for b in range(4): w[:, i, b, i, b] = -1
    wc, ws = packed(w.reshape(N, 128, 2048).astype(BF), rng)
    return {"x": x.astype(np.float32).reshape(N, 128, 4 * C).astype(BF), "u": u.reshape(N, 128, 512), "v": d["v"], "wc": wc, "ws": ws}
def setup_inputs_spread(rng):
    d = setup_inputs(rng)
    d["x"] = big(wide(rng, N, 128, 4 * C, cols=6))
    return d
def check_inputs(d):
    b = []
    for k in ("x", "u", "v"):
        a = np.abs(d[k].astype(np.float32))
        if not (np.isfinite(a).all() and ((a == 0) | (a >= 2.0 ** -30) & (a <= 2.0 ** 30)).all()): b.append("a value of " + k)
    none, least, most = [emit(mx_ref.quantize(np.full((128, 16), k, np.float32).astype(BF)))[1][0, 0] for k in (0.0, 2.0 ** -30, 2.0 ** 30)]
    for r in range(N):
        if ((d["wc"][r] == 0x7F) | (d["wc"][r] == 0xFF)).any(): b.append("wc: a code that is no number")
        s = mx_ref.live(d["ws"][r])
        if ((s != none) & ((s < least) | (s > most))).any(): b.append("ws: a scale out of range")
        if ((s == none) & ((d["wc"][r].reshape(16, 8, -1, 4) & 0x7F) != 0).any(axis=(1, 3))).any(): b.append("wc: a code that isn't zero under the scale of zeros")
    return b
def reference(x, u, v, wc, ws):
    qu = [mx_ref.quantize(u[r]) for r in range(N)]
    lay = [pk(wc[r], ws[r]) for r in range(N)]
    now = [x[r] for r in range(N)]
    for t in range(R):
        sent = [mx_ref.quantize(now[r]) for r in range(N)]
        p = [mx_ref.matmul(qu[r], sent[r]) for r in range(N)]
        came = decode(join(*sent)).astype(BF)
        made, places = [], []
        for r in range(N):
            s = (r + STEP[t]) % N
            lag = 1 + np.sum(p[r][1::16] > 0, axis=1) % 4
            e, m = match(p[r][::16], p[s][::16], lag)
            q = mx_ref.quantize(gcols(cut(came, s, 4 * C), (m + H) % C))
            own = gcols(now[r], e)
            h = tile([mx_ref.matmul(pick(lay[r], np.arange(128 * b, 128 * b + 128)), q) * np.float32(0.015625) + own[:, b::4].astype(np.float32) for b in range(4)])
            made.append(gput(now[r], e, h))
            places.append(e)
        now = made
    y, oe = np.zeros((N, 128, C), np.float32), np.zeros((N, 8, K), np.float32)
    oc, osc = np.zeros((N, 128, 4 * C), np.uint8), np.zeros((N, 16, C), np.uint8)
    for r in range(N):
        q = mx_ref.quantize(now[r])
        y[r] = mx_ref.matmul(mx_ref.quantize(v[r]), q)
        oe[r] = places[r]
        oc[r], osc[r] = emit(q)
    return {"y": y, "oe": oe, "oc": oc, "osc": osc}

@@ -1,0 +1,489 @@
+from concourse.bass import DstId, RemoteDMATransfer
+from concourse.mybir import dt, AluOpType, AxisListType, ActivationFunctionType
+
+C, K, R = 384, 192, 3
+STEP = [1, 3, 5]
+BIG = 1.0e29
+FAR = 2.0 ** 80
+HI = 16384.0
+NA, ND = 5, 3
+
+F32, BF, I32, U16, Q8, U8 = "float32", "bfloat16", "int32", "uint16", "float8_e4m3fn_x4", "uint8"
+SCRATCH = {"ps": ("psum", [128, 4096], F32)}
+for _n, _w, _d in (
+        [("xt%d" % t, 1536, BF) for t in range(4)] +
+        [("ut", 512, BF), ("vt", 512, BF), ("zt", 768, BF), ("et", 2048, BF), ("mumin", 384, BF), ("ones", 384, BF),
+         ("fl", 2 * ND * 384, BF), ("sc", 2 * ND * 384, BF), ("sj", 2 * NA * 384, BF), ("aj", 1536, BF), ("gt", 384, BF),
+         ("ci", 64, I32), ("cu", 64, U16), ("pi", 8, I32), ("pf", 8, F32), ("pat", 256, F32), ("tmp", 512, F32),
+         ("tmi", 32, I32), ("offc", 2, U16), ("offg", 28, U16), ("offr", 6, U16), ("offp", 24, U16),
+         ("offa", 24, U16), ("offt", 4, U16), ("offd", 24, U16), ("offj", 24, U16), ("offz", 12, U16), ("offx", 24, U16),
+         ("k24", 144, F32), ("mum", 64, F32), ("mask4", 64, F32), ("t3", 776, F32), ("t2", 384, F32),
+         ("nrow", 384, F32), ("mud", 192, F32), ("mu75", 80, F32), ("mu64", 64, F32),
+         ("rsb", 768, F32), ("g1", 448, F32), ("ts", 448, F32), ("aa", 1792, F32), ("ab", 1536, F32), ("dd", 1536, F32),
+         ("rr", 1536, F32), ("bb", 768, F32), ("tt", 768, F32), ("row", 384, F32), ("dc", 1536, F32), ("rs", 800, F32),
+         ("win", 776, F32), ("win2", 776, F32), ("srow", 384, F32), ("row1", 384, F32), ("row2", 384, F32),
+         ("dg", 192, F32), ("dg2", 384, F32), ("sm", 128, F32), ("sa", 32, F32), ("jm", 32, F32), ("s1", 128, F32),
+         ("s3", 64, F32), ("mm", 64, F32), ("mt", 64, F32), ("ff", 80, F32), ("ll", 80, F32), ("gm", 64, F32),
+         ("gs", 64, F32), ("yy", 80, F32), ("zz", 80, F32), ("ex", 80, F32), ("cm", 128, F32), ("yo", 384, F32)]):
+    SCRATCH[_n] = ("sbuf", [128, _w], _d)
+for _n, _w in ([("u", 128), ("uc", 16), ("so", 384), ("z", 192), ("e", 512), ("w", 512), ("v", 128)] +
+               [("lu%d" % t, 16) for t in range(1, R)] + [("sl%d" % t, 128) for t in range(R)] +
+               [("x%d" % t, 384 if t else 400) for t in range(R + 1)] + [("lx%d" % t, 384 if t else 400) for t in range(R)]):
+    SCRATCH["q" + _n] = ("sbuf", [128, _w], Q8)
+    SCRATCH["s" + _n + "p"] = ("sbuf", [128, _w], U8)
+
+SEMAPHORES = ["cv", "ca", "cp", "cg", "sent", "arru", "arr0", "arr1", "arr2"] + ["d%d" % i for i in range(16)]
+
+A = AluOpType
+ACT = ActivationFunctionType
+
+
+def rank_program(g, core, T, topo):
+    rank = T.rank_of(core)
+    if rank is None:
+        return
+    n_ranks = len(T.cores)
+    Q = {"v": g.vector, "a": g.scalar, "p": g.tensor, "g": g, "s": g.sync}
+    SEM = {"v": "cv", "a": "ca", "p": "cp", "g": "cg"}
+    count = {}
+    known = {e: {} for e in Q}
+    wrote, reads = {}, {}
+    ndma = [0]
+
+    def need(e, ev):
+        sem, val, clock = ev
+        if known[e].get(sem, 0) < val:
+            Q[e].wait_ge(T.sem[sem], val)
+            known[e][sem] = val
+            for s, x in clock.items():
+                if known[e].get(s, 0) < x:
+                    known[e][s] = x
+
+    def op(e, call, r=(), w=(), sem=None, inc=1):
+        evs = [wrote[k] for k in list(r) + list(w) if k in wrote]
+        for k in w:
+            evs += reads.get(k, [])
+        for ev in sorted(evs, key=lambda x: -x[1]):
+            need(e, ev)
+        sem = sem or SEM[e]
+        ins = call(Q[e])
+        if ins is not None:
+            ins.then_inc(T.sem[sem], inc)
+        count[sem] = count.get(sem, 0) + inc
+        ev = (sem, count[sem], dict(known[e]))
+        for k in r:
+            reads.setdefault(k, []).append(ev)
+        for k in w:
+            wrote[k] = ev
+            reads[k] = []
+        return ev
+
+    def dma(e, out, in_, r=(), w=()):
+        s = "d%d" % ndma[0]
+        ndma[0] += 1
+        op(e, lambda q: q.dma_start(out, in_), r, w, sem=s, inc=16)
+
+    def ts(out, in0, s1, s2, o0, o1=None, r=(), w=()):
+        if o1 is None:
+            op("v", lambda q: q.tensor_scalar(out, in0, s1, None, o0), r, w)
+        else:
+            op("v", lambda q: q.tensor_scalar(out, in0, s1, s2, o0, o1), r, w)
+
+    def tt(out, a, b, o, r=(), w=()):
+        op("v", lambda q: q.tensor_tensor(out, a, b, o), r, w)
+
+    def cp(out, in_, r=(), w=()):
+        op("v", lambda q: q.tensor_copy(out, in_), r, w)
+
+    def acp(out, in_, r=(), w=()):
+        op("a", lambda q: q.activation(out, in_, ACT.Copy), r, w)
+
+    def ms(ap, val, w):
+        op("v", lambda q: q.memset(ap, val), (), w)
+
+    def scan(out, d0, d1, init, o0, o1, r=(), w=()):
+        op("v", lambda q: q.tensor_tensor_scan(out, d0, d1, init, o0, o1), r, w)
+
+    def red(out, in_, o, r=(), w=()):
+        op("v", lambda q: q.tensor_reduce(out, in_, AxisListType.X, o), r, w)
+
+    def tr(out, in_, r=(), w=()):
+        op("v", lambda q: q.transpose(out, in_), r, w)
+
+    def iota(out, pat, base, w, cm=0, f=True):
+        if f:
+            op("g", lambda q: q.iota(out, pat, base, cm, allow_small_or_imprecise_dtypes=True), (), w)
+        else:
+            op("g", lambda q: q.iota(out, pat, base, cm), (), w)
+
+    def quant(name, a, z, tile, r, tag=""):
+        op("v", lambda q: q.quantize_mx(T["q" + name][:, a:z], T["s" + name + "p"][:, a:z], tile), r, ["q" + name + tag, "s" + name + tag])
+
+    def mm(bank, st, a, mv, n):
+        op("p", lambda q: q.matmul_mx(T.ps[:, 512 * bank:512 * bank + n], T["q" + st][:, a:a + 128], T["s" + st + "p"][:, a:a + 128],
+                                      T["q" + mv][:, 0:n], T["s" + mv + "p"][:, 0:n], True, True),
+           ["q" + st, "s" + st, "q" + mv, "s" + mv, "q" + mv + "h", "s" + mv + "h"], ["b%d" % bank])
+
+    def pick(dst, src, off, key, d=slice(None), s=slice(None), tag=""):
+        cp(T["q" + dst][:, d].bitcast(dt.uint32), T["q" + src][:, s].bitcast(dt.uint32).indirect(off), ["q" + src, key], ["q" + dst + tag])
+        acp(T["s" + dst + "p"][:, d], T["s" + src + "p"][:, s].indirect(off), ["s" + src, key], ["s" + dst + tag])
+
+    def bank(b, a=0, z=C, step=1):
+        return T.ps[:, 512 * b + a:512 * b + z:step]
+
+    askers = [T.cores[(rank - s) % n_ranks] for s in STEP]
+    mask = topo.mask(core, askers[0])
+    for c in askers:
+        mask &= topo.mask(core, c)
+    n_eng = bin(mask).count("1")
+
+    def remote(call, r):
+        op("g", call, r, (), sem="sent", inc=n_eng)
+
+    def post(t, kind, cols, r):
+        rid, pid = topo.addr(askers[t])[:2]
+        arr = "arr%d" % t
+        if kind == "q":
+            dst, src = T["qlx%d" % t][:, cols].bitcast(dt.uint8), T["qx%d" % t][:, cols].bitcast(dt.uint8)
+        else:
+            dst, src = T["slx%dp" % t][:, cols], T["sx%dp" % t][:, cols]
+
+        def call(q):
+            q.remote_dma(dst, src, T.sem[arr], T.sem.sent, pid, rid, mask)
+        remote(call, r)
+        count[arr] = count.get(arr, 0) + n_eng
+        wrote["qlx%d" % t] = wrote["slx%d" % t] = (arr, count[arr], {})
+
+    def post_u():
+        ids = [DstId(rid=topo.addr(c)[0], pnc=topo.addr(c)[1]) for c in askers[1:]]
+
+        def codes(q):
+            q.remote_dma_fused([RemoteDMATransfer(dst_ids=ids, dma_engine_mask=mask, remote_sem=T.sem.arru, srcs=[T.quc[:].bitcast(dt.uint8)],
+                                                  dsts=[T["qlu%d" % t][:].bitcast(dt.uint8) for t in range(1, R)])], local_sem=T.sem.sent)
+
+        def plane(q):
+            q.remote_dma_fused([RemoteDMATransfer(dst_ids=ids, dma_engine_mask=mask, remote_sem=T.sem.arru, srcs=[T.sucp[:]],
+                                                  dsts=[T["slu%dp" % t][:] for t in range(1, R)])], local_sem=T.sem.sent)
+        remote(codes, ["quc"])
+        remote(plane, ["suc"])
+        count["arru"] = 2 * (R - 1) * n_eng
+        for t in range(1, R):
+            wrote["qlu%d" % t] = wrote["slu%d" % t] = ("arru", 2 * (R - 1) * n_eng, {})
+
+    dma("s", T.ut[:], T.u[:], (), ["ut"])
+    dma("a", T.xt0[:, 0:768], T.x[:, 0:768], (), ["x0a"])
+    dma("s", T.xt0[:, 768:1536], T.x[:, 768:1536], (), ["x0b"])
+
+    pat, pf, k24, tmp = T.pat, T.pf, T.k24, T.tmp
+    iota(T.pi[:, 0:1], [[0, 1]], 0, ["pi0"], cm=1, f=False)
+    iota(T.pi[:, 1:2], [[0, 1]], 0, ["pi1"], cm=16, f=False)
+    iota(T.ci[:, 0:16], [[16, 2], [32, 4], [0, 2]], 0, ["ci0"], f=False)
+    iota(T.ci[:, 16:24], [[16, 8]], 1, ["ci1"], f=False)
+    iota(T.ci[:, 24:32], [[1, 8]], 0, ["ci2"], f=False)
+    iota(T.ci[:, 32:44], [[64, 6], [0, 2]], 63, ["ci3"], f=False)
+    iota(pat[:, 0:28], [[2, 14], [0, 2]], -4, ["pa0"])
+    iota(pat[:, 28:56], [[0, 14], [C, 2]], 0, ["pa1"])
+    iota(pat[:, 56:80], [[16, 24]], 0, ["pa2"])
+    iota(pat[:, 80:104], [[0, 6], [16, 4]], 0, ["pa3"])
+    iota(k24[:, 0:24], [[64, 6], [0, 4]], 0, ["s64"])
+    iota(pat[:, 104:110], [[32, 6]], 0, ["pa4"])
+    iota(pat[:, 112:144], [[16, 2], [0, 16]], 0, ["pa5"])
+    iota(pat[:, 144:176], [[0, 2], [1, 16]], 0, ["pa6"])
+    iota(pat[:, 176:200], [[1, 24]], 193, ["pa7"])
+
+    ms(T.ones[:], 1.0, ["ones"])
+    ms(T.mumin[:], 0.0, ["mumin"])
+    ts(T.pi[:, 2:3], T.pi[:, 1:2], 127, None, A.bitwise_and, r=["pi1"], w=["pi2"])
+    ts(T.pi[:, 4:5], T.pi[:, 0:1], 15, None, A.bitwise_and, r=["pi0"], w=["pi4"])
+    ts(T.pi[:, 5:6], T.pi[:, 0:1], 16, None, A.bitwise_and, r=["pi0"], w=["pi5"])
+    ts(T.pi[:, 6:7], T.pi[:, 0:1], 127, None, A.bitwise_and, r=["pi0"], w=["pi6"])
+    ms(T.mu75[:], 1.0, ["mu75"])
+    ms(T.mu64[:], 1.0, ["mu64"])
+    cp(T.offc[:, 0:1], T.pi[:, 2:3], ["pi2"], ["offc"])
+    cp(pf[:, 0:3], T.pi[:, 4:7], ["pi4", "pi5", "pi6"], ["pf"])
+    cf, h16, pp, c24 = pf[:, 0:1], pf[:, 1:2], pf[:, 2:3], pf[:, 3:4]
+    scan(T.t3[:, 0:193], T.ones[:, 0:193], T.ones[:, 0:193], -1.0, A.mult, A.add, ["ones"], ["t3a"])
+    ms(T.mumin[:, 0:C:64], BIG, ["mumin"])
+    ms(T.ff[:], 0.0, ["ff0", "ff1", "ff2"])
+    ms(T.rs[:, 0:800:200], 0.0, ["rs0"])
+    ms(T.yy[:], 0.0, ["yya", "yyb"])
+    ms(T.zz[:], 0.0, ["zza", "zzb"])
+    ms(T.cm[:, 0:48], 0.0, ["out"])
+    ms(T.mu75[:, 0:75:25], 0.0, ["mu75"])
+    ms(T.mu64[:, 0:64:16], 0.0, ["mu64"])
+    ts(pf[:, 3:4], cf, 24.0, None, A.mult, r=["pf"], w=["c24"])
+    ts(pf[:, 4:5], h16, 0.0625, None, A.mult, r=["pf"], w=["hh"])
+    cp(T.cu[:, 0:44], T.ci[:, 0:44], ["ci0", "ci1", "ci2", "ci3"], ["cu"])
+
+    quant("u", 0, 128, T.ut[:], ["ut"])
+    ms(T.et[:, 0:512], 0.0, ["et0"])
+    pick("x0", "u", T.offc[:, 0:1], "offc", d=slice(C, C + 16), tag="u")
+    quant("x0", 0, C, T.xt0[:], ["x0a", "x0b"])
+    post(0, "q", slice(None), ["qx0", "qx0u"])
+    post(0, "s", slice(None), ["sx0", "sx0u"])
+    pick("so", "u", T.cu[:, 0:24], "cu")
+    ts(tmp[:, 0:28], pat[:, 0:28], c24, pf[:, 4:5], A.add, A.add, r=["pa0", "c24", "hh"], w=["t0"])
+    ts(k24[:, 24:48], pat[:, 56:80], cf, 192.0, A.add, A.add, r=["pa2", "pf"], w=["base"])
+    ts(tmp[:, 32:60], tmp[:, 0:28], 0.0, float(C), A.is_lt, A.mult, r=["t0"], w=["t1"])
+    tt(tmp[:, 64:92], tmp[:, 0:28], pat[:, 28:56], A.add, r=["t0", "pa1"], w=["t2_"])
+    ts(tmp[:, 128:152], pat[:, 80:104], cf, 0.0, A.add, A.is_equal, r=["pa3", "pf"], w=["t4"])
+    tt(tmp[:, 96:124], tmp[:, 64:92], tmp[:, 32:60], A.add, r=["t1", "t2_"], w=["t3_"])
+    ts(k24[:, 48:72], tmp[:, 128:152], -64.0, 1.0, A.mult, A.add, r=["t4"], w=["cj"])
+    cp(T.offg[:], tmp[:, 96:124], ["t3_"], ["offg"])
+    pick("uc", "u", T.offc[:, 0:1], "offc")
+    post_u()
+
+    iota(tmp[:, 192:384], [[0, 12], [1, 16]], 0, ["jm16"])
+    iota(k24[:, 72:96], [[0, 4], [64, 6]], 0, ["k64s"])
+    iota(T.t2[:], [[1, 6], [6, 64]], 8, ["t2"])
+    iota(T.t2[:, 63:C:64], [[1, 6]], 2, ["t2"])
+    iota(T.t2[:, 318:C:64], [[1, 2]], 0, ["t2"])
+    iota(T.nrow[:], [[1, 24], [24, 16]], 0, ["nrow"])
+
+    def late_loads():
+        need("s", ("sent", count["sent"], {}))
+        dma("s", T.qw[:].bitcast(dt.uint8), T.wc[:], (), ["qw"])
+        dma("s", T.swp[:], T.ws[:], (), ["sw"])
+        dma("s", T.vt[:], T.v[:], (), ["vt"])
+
+    def constants_b():
+        ts(T.offr[:], pat[:, 104:110], cf, h16, A.add, A.add, r=["pa4", "pf"], w=["offr"])
+        ms(T.et[:, 512:2048], 0.0, ["et1", "et2", "et3"])
+        ts(T.mum[:, 0:32], pat[:, 112:144], h16, None, A.is_equal, r=["pa5", "pf"], w=["mu_u"])
+        for b in range(4):
+            ts(T.et[:, 512 * b + b:512 * b + 512:4], T.t3[:, 0:128], pp, None, A.is_equal, r=["t3a", "pf"], w=["et%d" % b])
+        ts(T.mum[:, 32:64], pat[:, 112:144], h16, BIG, A.not_equal, A.mult, r=["pa5", "pf"], w=["mu_t"])
+        quant("e", 0, 512, T.et[:], ["et0", "et1", "et2", "et3"])
+        ts(T.mask4[:, 0:32], pat[:, 144:176], cf, -1.0, A.is_ge, A.mult, r=["pa6", "pf"], w=["m4a"])
+        ts(T.mask4[:, 32:64], pat[:, 144:176], cf, None, A.is_lt, r=["pa6", "pf"], w=["m4b"])
+        ts(k24[:, 96:144:2], pat[:, 176:200], c24, None, A.add, r=["pa7", "c24"], w=["n193"])
+        ts(pf[:, 5:6], cf, 15.0, 1.0 / HI, A.is_equal, A.max, r=["pf"], w=["kap"])
+        ts(pf[:, 6:7], cf, 1.0, None, A.add, r=["pf"], w=["c1"])
+        ts(tmp[:, 0:24], k24[:, 24:48], -203.5, 1.0 / 24.0, A.add, A.mult, r=["base"], w=["t0"])
+        ts(tmp[:, 32:56], k24[:, 24:48], -192.0, 16.0, A.add, A.mult, r=["base"], w=["t1"])
+        cp(T.tmi[:, 0:24], tmp[:, 0:24], ["t0"], ["tmi"])
+        ts(T.dg[:], tmp[:, 192:384], cf, None, A.not_equal, r=["jm16", "pf"], w=["dg"])
+        ts(tmp[:, 64:88], T.tmi[:, 0:24], -383.0, None, A.mult, r=["tmi"], w=["t2_"])
+        ts(T.dg2[:, 0:192], tmp[:, 192:384], pf[:, 6:7], HI - 1.0, A.is_equal, A.mult, r=["jm16", "c1"], w=["dg2a"])
+        tt(tmp[:, 96:120], tmp[:, 64:88], tmp[:, 32:56], A.add, r=["t1", "t2_"], w=["t3_"])
+        tt(T.mud[:], T.dg[:], T.dg2[:, 0:192], A.add, r=["dg", "dg2a"], w=["mud"])
+        cp(T.offp[:], tmp[:, 96:120], ["t3_"], ["offp"])
+        pick("sl0", "lx0", T.cu[:, 24:32], "cu", s=slice(C, C + 16))
+        ms(T.t3[:, 193:776], 0.0, ["t3b"])
+
+    def own_side(t):
+        x = "x%d" % t
+        mm(3, "so", 256, x, C)
+        mm(1, "so", 0, x, C)
+        mm(2, "so", 128, x, C)
+        sm = T.sm
+        ts(T.gt[:], bank(3), 0.0, None, A.is_gt, r=[], w=["gt", "b3"])
+        acp(T.rsb[:, 0:C], bank(1), [], ["rsb0", "b1"])
+        acp(T.rsb[:, C:2 * C], bank(2), [], ["rsb1", "b2"])
+        acp(T.g1[:], T.rsb[:].indirect(T.offg[:]), ["rsb0", "rsb1", "offg"], ["g1"])
+        red(sm[:, 0:1], T.gt[:], A.add, ["gt"], ["cnt"])
+        ts(T.tmi[:, 24:25], sm[:, 0:1], 64.0, None, A.mult, r=["cnt"], w=["cnti"])
+        ts(T.tmi[:, 26:27], T.tmi[:, 24:25], 192, None, A.bitwise_and, r=["cnti"], w=["ami"])
+        cp(sm[:, 1:2], T.tmi[:, 26:27], ["ami"], ["am"])
+        ts(sm[:, 8:32], k24[:, 0:24], sm[:, 1:2], None, A.is_le, r=["s64", "am"], w=["car"])
+        tt(sm[:, 32:56], sm[:, 8:32], k24[:, 48:72], A.mult, ["car", "cj"], ["car2"])
+        tt(sm[:, 56:80], k24[:, 24:48], sm[:, 32:56], A.subtract, ["car2", "base"], ["car3"])
+        ts(T.offa[:], sm[:, 56:80], sm[:, 1:2], None, A.subtract, r=["car3", "am"], w=["offa"])
+        tr(T.ts[:], T.g1[:], ["g1"], ["ts"])
+
+    def argmin(i):
+        for k in range(6 * i, 6 * i + 6):
+            op("a", lambda q: q.activation(T.aj[:, 64 * k:64 * k + 64], T.rr[:, 64 * k:64 * k + 64], ACT.Sign,
+                                           bias=T.rr[:, 64 * k + 63:64 * k + 64], scale=-1.0, accum_out=T.jm[:, k:k + 1]),
+               ["rr%d" % i], ["aj%d" % k, "jm%d" % k])
+
+    def one_round(t):
+        lx = "lx%d" % t
+        mm(0, "sl%d" % t, 0, lx, C)
+        for b in range(4):
+            mm(4 + b, "e", 128 * b, lx, C)
+
+        def apart(k0, k1, i):
+            for kk in range(k0, k1):
+                op("a", lambda q: q.activation(T.aa[:, 64 * kk:64 * kk + 64], bank(0, (kk + 2) % 6, C, 6), ACT.Abs,
+                                               bias=T.ts[:, 16 * kk:16 * kk + 1], scale=-1.0), ["ts", "b0"], ["aa%d" % kk])
+            if i:
+                acp(T.ab[:, C * i:C * i + C], T.aa[:, C * i + 256:C * i + 640], ["aa%d" % kk for kk in range(6 * i + 4, 6 * i + 10)], ["ab%d" % i])
+
+        def larger(i):
+            a = C * i
+            if i == 0:
+                for k in range(6):
+                    tt(T.dd[:, 64 * k:64 * k + 64], T.aa[:, 0:64 * k + 256].indirect(T.offa[:, 4 * k:4 * k + 4]),
+                       T.aa[:, 64 * k + 256:64 * k + 320], A.max, ["aa%d" % kk for kk in range(k + 5)] + ["offa"], ["dd0_%d" % k])
+            else:
+                tt(T.dd[:, a:a + C], T.aa[:, a:a + 576].indirect(T.offa[:]), T.ab[:, a:a + C], A.max,
+                   ["aa%d" % kk for kk in range(6 * i, 6 * i + 9)] + ["offa", "ab%d" % i], ["dd%d_0" % i])
+
+        def least(i):
+            a = C * i
+            scan(T.rr[:, a:a + C], T.mumin[:], T.dd[:, a:a + C], 0.0, A.add, A.min, ["dd%d_%d" % (i, k) for k in range(6)] + ["mumin"], ["rr%d" % i])
+
+        def wide(i, f=acp, a=0, z=12, tag=""):
+            f(T.bb[:, 192 * i + 16 * a:192 * i + 16 * z], T.rr[:, C * i:C * i + C].indirect(T.cu[:, 32 + a:32 + z]),
+              ["rr%d" % i, "cu"], ["bb%d%s" % (i, tag)])
+
+        def turn(i):
+            tr(T.tt[:, 192 * i:192 * i + 192], T.bb[:, 192 * i:192 * i + 192], ["bb%d" % i, "bb%dv" % i], ["tt%d" % i])
+
+        def rowp(i):
+            acp(T.row[:, 96 * i:96 * i + 96], T.tt[:, 192 * i:192 * i + 192].indirect(T.offr[:]), ["tt%d" % i, "offr"], ["row%d" % i])
+
+        def dm(k0, k1):
+            return T.rr[:, 64 * k0 + 63:64 * k1:64]
+
+        s1, s3 = T.s1, T.s3
+        rows, rrs = ["row%d" % i for i in range(4)], ["rr%d" % i for i in range(4)]
+        mn, mx, lo, hi, m2 = (s3[:, 8 * i:8 * i + 8] for i in range(5))
+        apart(0, 10, 0); apart(10, 16, 1); apart(16, 22, 2)
+        larger(0); least(0); larger(1)
+        wide(0); least(1); turn(0); apart(22, 28, 3); wide(1); rowp(0)
+        larger(2); turn(1); least(2)
+        argmin(0); wide(2); rowp(1); argmin(1)
+        larger(3)
+        tt(mn, dm(0, 8), dm(8, 16), A.min, rrs[:3], ["mn"])
+        tt(mx, dm(0, 8), dm(8, 16), A.max, rrs[:3], ["mx"])
+        turn(2); least(3)
+        rowp(2); wide(3, acp, 0, 6); wide(3, cp, 6, 12, "v")
+        tt(m2, mx, dm(16, 24), A.min, ["mx"] + rrs, ["m2"])
+        turn(3); rowp(3)
+        cand, wv, dcol = s1[:, 0:16], s1[:, 16:32], s1[:, 32:56]
+        tt(s1[:, 0:8], mn, m2, A.max, ["mn", "m2"], ["cand%d" % i for i in range(8)])
+        tt(lo, mn, dm(16, 24), A.min, ["mn"] + rrs, ["lo"])
+        tt(hi, mx, dm(16, 24), A.max, ["mx"] + rrs, ["hi"])
+
+        def count_a(p, i):
+            j = NA * p + i
+            op("a", lambda q: q.activation(T.sj[:, C * j:C * j + C], T.row[:], ACT.Sign, bias=s1[:, 8 * p + i:8 * p + i + 1], scale=-1.0,
+                                           accum_out=T.sa[:, 8 * p + i:8 * p + i + 1]), rows + ["cand%d" % (8 * p + i)], ["sj%d" % j, "sa%d" % (8 * p + i)])
+
+        def below(p, i):
+            j, k = ND * p + i, 8 * p + NA + i
+            ts(T.fl[:, C * j:C * j + C], T.row[:], s1[:, k:k + 1], -FAR, A.is_lt, A.mult, r=rows + ["cand%d" % k], w=["fl%d" % j])
+
+        def total(p, i):
+            j = ND * p + i
+            scan(T.sc[:, C * j:C * j + C], T.ones[:], T.fl[:, C * j:C * j + C], (K - 0.5) * FAR, A.mult, A.add, ["fl%d" % j, "ones"], ["sc%d" % j])
+
+        def side_a(k0, k1):
+            ts(s1[:, 16 + k0:16 + k1], T.sa[:, k0:k1], -FAR, None, A.mult, r=["sa%d" % k for k in range(k0, k1)], w=["wv%d" % k for k in range(k0, k1)])
+
+        def side_d(p):
+            cp(s1[:, 16 + 8 * p + NA:24 + 8 * p], T.sc[:, C * ND * p + C - 1:C * ND * (p + 1):C], ["sc%d" % (ND * p + i) for i in range(ND)],
+               ["wv%d" % (8 * p + NA + i) for i in range(ND)])
+
+        def cap(k0, k1, w=None, r=None):
+            tt(s3[:, 40 + k0:40 + k1], s3[:, 24 + k0:24 + k1], s1[:, 16 + k0:16 + k1] if w is None else w, A.min,
+               ["hi"] + (r or ["wv%d" % k for k in range(k0, k1)]), ["cap%d" % k for k in range(k0, k1)])
+
+        def next_one(k0, k1):
+            tt(s1[:, 8 + k0:8 + k1], s3[:, 40 + k0:40 + k1], s3[:, 16 + k0:16 + k1], A.max,
+               ["lo"] + ["cap%d" % k for k in range(k0, k1)], ["cand%d" % (8 + k) for k in range(k0, k1)])
+
+        for i in range(NA):
+            count_a(0, i)
+        below(0, 0); below(0, 1); total(0, 0); below(0, 2); total(0, 1); side_a(0, 3); total(0, 2); cap(0, 3)
+        cp(dcol, dm(0, 24), rrs, ["dcol"])
+        next_one(0, 3)
+        cap(NA, 8, T.sc[:, C - 1:C * ND:C], ["sc%d" % i for i in range(ND)])
+        side_d(0); next_one(NA, 8)
+        for i in range(3):
+            count_a(1, i)
+        side_a(3, NA); below(1, 0); cap(3, NA); below(1, 1); next_one(3, NA)
+        for i in range(3, NA):
+            count_a(1, i)
+        total(1, 0); below(1, 2); total(1, 1); total(1, 2)
+        argmin(2); argmin(3)
+        side_d(1); side_a(8, 8 + NA)
+        cw = ["cand%d" % k for k in range(16)] + ["wv%d" % k for k in range(16)]
+        tt(s1[:, 56:72], cand, wv, A.min, cw, ["du"])
+        tt(s1[:, 72:88], cand, wv, A.max, cw, ["dt"])
+        red(s1[:, 96:97], s1[:, 56:72], A.max, ["du"], ["up"])
+        red(s1[:, 97:98], s1[:, 72:88], A.min, ["dt"], ["tp"])
+        ts(T.mm[:, 0:32], T.mum[:, 0:32], s1[:, 96:97], None, A.mult, r=["mu_u", "up"], w=["mma"])
+        ts(T.mm[:, 32:64], T.mum[:, 32:64], s1[:, 97:98], None, A.max, r=["mu_t", "tp"], w=["mmb"])
+        tr(T.mt[:], T.mm[:], ["mma", "mmb"], ["mt"])
+        red(s1[:, 98:99], T.mt[:, 0:32], A.max, ["mt"], ["uu"])
+        red(s1[:, 99:100], T.mt[:, 32:64], A.min, ["mt"], ["tu"])
+        ts(T.ff[:, 1:25], dcol, s1[:, 98:99], None, A.is_lt, r=["dcol", "uu"], w=["ff0"])
+        ts(T.ff[:, 26:50], dcol, s1[:, 98:99], None, A.is_le, r=["dcol", "uu"], w=["ff1"])
+        ts(T.ff[:, 51:75], dcol, s1[:, 99:100], None, A.is_le, r=["dcol", "tu"], w=["ff2"])
+        for b in range(2):
+            acp(T.dc[:, C * b:C * b + C], bank(4 + b), [], ["dc%d" % b, "b%d" % (4 + b)])
+        scan(T.ll[:, 0:75], T.mu75[:, 0:75], T.ff[:, 0:75], 0.0, A.mult, A.add, ["ff0", "ff1", "ff2", "mu75"], ["ll"])
+        cp(T.offt[:, 0:2], T.ll[:, 24:50:25], ["ll"], ["ofta"])
+        cp(T.offt[:, 2:4], T.ll[:, 49:75:25], ["ll"], ["oftb"])
+        tt(T.sm[:, 80:104], k24[:, 72:96], T.jm[:, 0:24], A.subtract, ["k64s"] + ["jm%d" % k for k in range(24)], ["jj"])
+        tt(T.gm[:], T.t3[:, 0:32].indirect(T.offt[:]), T.mask4[:], A.mult, ["t3a", "ofta", "oftb", "m4a", "m4b"], ["gm"])
+        cp(T.offj[:], T.sm[:, 80:104], ["jj"], ["offj"])
+        acp(T.srow[:], T.t2[:].indirect(T.offj[:]), ["t2", "offj"], ["srow"])
+        for b in range(2, 4):
+            acp(T.dc[:, C * b:C * b + C], bank(4 + b), [], ["dc%d" % b, "b%d" % (4 + b)])
+        scan(T.gs[:], T.mu64[:], T.gm[:], 0.0, A.mult, A.add, ["gm", "mu64"], ["gs"])
+        ts(T.yy[:, 0:75:3], T.ll[:, 0:25], T.gs[:, 15:16], float(K), A.add, A.add, r=["ll", "gs"], w=["yya"])
+        ts(T.zz[:, 1:75:3], T.ll[:, 25:50], T.gs[:, 47:48], None, A.add, r=["ll", "gs"], w=["zza"])
+        ts(T.yy[:, 1:75:3], T.ll[:, 25:50], T.gs[:, 31:32], float(K), A.add, A.add, r=["ll", "gs"], w=["yyb"])
+        ts(T.zz[:, 2:75:3], T.ll[:, 50:75], T.gs[:, 63:64], None, A.add, r=["ll", "gs"], w=["zzb"])
+        scan(T.ex[:, 0:75], T.zz[:, 0:75], T.yy[:, 0:75], 0.0, A.min, A.max, ["yya", "yyb", "zza", "zzb"], ["cum"])
+        cm = T.cm
+        tt(cm[:, 1:48:2], T.ex[:, 2:74:3], T.ex[:, 5:75:3], A.is_equal, ["cum"], ["out"])
+        cp(k24[:, 97:144:2], T.ex[:, 5:75:3], ["cum"], ["out2"])
+        scan(cm[:, 64:112], cm[:, 0:48], k24[:, 96:144], 0.0, A.mult, A.add, ["out", "out2", "n193"], ["dst"])
+        cp(T.offd[:], cm[:, 65:112:2], ["dst"], ["offd"])
+        cp(T.win[:].indirect(T.offd[:]), T.srow[:], ["srow", "offd"], ["win"])
+        acp(T.row1[:], T.t3[:].indirect(T.offd[:]), ["t3a", "t3b", "offd"], ["row1_"])
+        acp(T.row2[:], T.row1[:].indirect(T.offp[:]), ["row1_", "offp"], ["row2_"])
+        scan(T.dg[:], T.mud[:], T.win[:, 1:193], 0.0, A.mult, A.add, ["win", "mud"], ["dg"])
+        ts(T.offz[:], T.dg[:, 15:192:16], pf[:, 5:6], None, A.mult, r=["dg", "kap"], w=["offz"])
+        for b in range(4):
+            (cp if b < 2 else acp)(T.zt[:, b:768:4], T.dc[:, C * b:C * b + C].indirect(T.offz[:]), ["dc%d" % b, "offz"], ["zt%d" % b])
+        quant("z", 0, K, T.zt[:], ["zt%d" % b for b in range(4)])
+        scan(T.dg2[:, 0:192], T.mud[:], T.row2[:, 0:192], 0.0, A.mult, A.add, ["row2_", "mud"], ["dg2a"])
+        scan(T.dg2[:, 192:C], T.mud[:], T.row2[:, 192:C], 0.0, A.mult, A.add, ["row2_", "mud"], ["dg2b"])
+        ts(T.offx[:, 0:12], T.dg2[:, 15:K:16], pf[:, 5:6], None, A.mult, r=["dg2a", "kap"], w=["offx0"])
+        ts(T.offx[:, 12:24], T.dg2[:, K + 15:C:16], pf[:, 5:6], None, A.mult, r=["dg2b", "kap"], w=["offx1"])
+        for b in range(4):
+            mm(b, "w", 128 * b, "z", K)
+            op("a", lambda q: q.activation(T.rs[:, 200 * b + 1:200 * b + 193], bank(b, 0, K), ACT.Copy, scale=0.015625),
+               [], ["rs_%d" % b, "b%d" % b])
+        old = ["x0a", "x0b"] if t == 0 else ["xt%d_%d" % (t, b) for b in range(8)]
+        xo, xn, nx = T["xt%d" % t], T["xt%d" % (t + 1)], "x%d" % (t + 1)
+        halves = [(0, 12), (12, 24)] if t + 1 < R else [(0, 24)]
+        for h, (a, z) in enumerate(halves):
+            keys = ["xt%d_%d" % (t + 1, 4 * h + b) for b in range(4)]
+            for b in range(4):
+                tt(xn[:, 64 * a + b:64 * z:4], T.rs[:, 200 * b:200 * b + 193].indirect(T.offx[:, a:z]), xo[:, 64 * a + b:64 * z:4], A.add,
+                   ["rs0", "rs_%d" % b, "offx0"] + (["offx1"] if z > 12 else []) + old, [keys[b]])
+            quant(nx, 16 * a, 16 * z, xn[:, 64 * a:64 * z], keys, tag="h" if h else "")
+            if t + 1 < R:
+                post(t + 1, "q", slice(16 * a, 16 * z), ["q" + nx + ("h" if h else "")])
+        if t + 1 < R:
+            post(t + 1, "s", slice(None), ["s" + nx, "s" + nx + "h"])
+
+    late_loads()
+    for t in range(R):
+        own_side(t)
+        if t == 0:
+            constants_b()
+        else:
+            pick("sl%d" % t, "lu%d" % t, T.cu[:, 24:32], "cu")
+        if t == 1:
+            quant("v", 0, 128, T.vt[:], ["vt"])
+        one_round(t)
+
+    mm(4, "v", 0, "x3", C)
+    dma("s", T.oc[:], T.qx3[:].bitcast(dt.uint8), ["qx3"], [])
+    for k in range(4):
+        dma("s", T.osc[4 * k:4 * k + 4, :], T.sx3p[32 * k:32 * k + 4, :], ["sx3"], [])
+    acp(T.yo[:], bank(4), [], ["yo", "b4"])
+    dma("a", T.y[:], T.yo[:], ["yo"], [])
+    cp(T.win2[:].indirect(T.offd[:]), T.nrow[:], ["nrow", "offd"], ["win2"])
+    dma("s", T.oe[:], T.win2[0:128:16, 1:193], ["win2"], [])
+    for s in SEMAPHORES:
+        if count.get(s, 0):
+            need("g", (s, count[s], {}))

@@ -6,6 +6,7 @@ STEP = [1, 3, 5]
 BIG = 1.0e29
 FAR = 2.0 ** 80
 HI = 16384.0
+NI = 2
 NA, ND = 5, 3
 
 F32, BF, I32, U16, Q8, U8 = "float32", "bfloat16", "int32", "uint16", "float8_e4m3fn_x4", "uint8"
@@ -18,7 +19,7 @@ for _n, _w, _d in (
          ("tmi", 32, I32), ("offc", 2, U16), ("offg", 28, U16), ("offr", 6, U16), ("offp", 24, U16),
          ("offa", 24, U16), ("offt", 4, U16), ("offd", 24, U16), ("offj", 24, U16), ("offz", 12, U16), ("offx", 24, U16),
          ("k24", 144, F32), ("mum", 64, F32), ("mask4", 64, F32), ("t3", 776, F32), ("t2", 384, F32),
-         ("nrow", 384, F32), ("mud", 192, F32), ("mu75", 80, F32), ("mu64", 64, F32),
+         ("nrow", 384, F32), ("mud", 192, F32), ("mu75", 80, F32), ("mu64", 64, F32), ("eab", 128, F32),
          ("rsb", 768, F32), ("g1", 448, F32), ("ts", 448, F32), ("aa", 1792, F32), ("ab", 1536, F32), ("dd", 1536, F32),
          ("rr", 1536, F32), ("bb", 768, F32), ("tt", 768, F32), ("row", 384, F32), ("dc", 1536, F32), ("rs", 800, F32),
          ("win", 776, F32), ("win2", 776, F32), ("srow", 384, F32), ("row1", 384, F32), ("row2", 384, F32),
@@ -192,12 +193,16 @@ def rank_program(g, core, T, topo):
     iota(pat[:, 176:200], [[1, 24]], 193, ["pa7"])
 
     ms(T.ones[:], 1.0, ["ones"])
+    for i in range(6):
+        a_, z_ = C * i, min(C * i + C, 2048)
+        op("a", lambda q: q.activation(T.et[:, a_:z_], T.ones[:, 0:z_ - a_], ACT.Copy, scale=0.0), ["ones"], ["etz%d" % i])
     ms(T.mumin[:], 0.0, ["mumin"])
     ts(T.pi[:, 2:3], T.pi[:, 1:2], 127, None, A.bitwise_and, r=["pi1"], w=["pi2"])
     ts(T.pi[:, 4:5], T.pi[:, 0:1], 15, None, A.bitwise_and, r=["pi0"], w=["pi4"])
     ts(T.pi[:, 5:6], T.pi[:, 0:1], 16, None, A.bitwise_and, r=["pi0"], w=["pi5"])
     ts(T.pi[:, 6:7], T.pi[:, 0:1], 127, None, A.bitwise_and, r=["pi0"], w=["pi6"])
     ms(T.mu75[:], 1.0, ["mu75"])
+    ms(pf[:, 7:8], 1.0, ["one"])
     ms(T.mu64[:], 1.0, ["mu64"])
     cp(T.offc[:, 0:1], T.pi[:, 2:3], ["pi2"], ["offc"])
     cp(pf[:, 0:3], T.pi[:, 4:7], ["pi4", "pi5", "pi6"], ["pf"])
@@ -216,12 +221,15 @@ def rank_program(g, core, T, topo):
     cp(T.cu[:, 0:44], T.ci[:, 0:44], ["ci0", "ci1", "ci2", "ci3"], ["cu"])
 
     quant("u", 0, 128, T.ut[:], ["ut"])
-    ms(T.et[:, 0:512], 0.0, ["et0"])
     pick("x0", "u", T.offc[:, 0:1], "offc", d=slice(C, C + 16), tag="u")
     quant("x0", 0, C, T.xt0[:], ["x0a", "x0b"])
     post(0, "q", slice(None), ["qx0", "qx0u"])
     post(0, "s", slice(None), ["sx0", "sx0u"])
+    op("a", lambda q: q.activation(T.eab[:], T.t3[:, 0:128], ACT.Abs, bias=pp, scale=-1.0), ["t3a", "pf"], ["eab"])
     pick("so", "u", T.cu[:, 0:24], "cu")
+    for b in range(4):
+        op("a", lambda q: q.activation(T.et[:, 512 * b + b:512 * b + 512:4], T.eab[:], ACT.Relu, bias=pf[:, 7:8], scale=-1.0),
+           ["eab", "one"] + ["etz%d" % i for i in range(6)], ["et%d" % b])
     ts(tmp[:, 0:28], pat[:, 0:28], c24, pf[:, 4:5], A.add, A.add, r=["pa0", "c24", "hh"], w=["t0"])
     ts(k24[:, 24:48], pat[:, 56:80], cf, 192.0, A.add, A.add, r=["pa2", "pf"], w=["base"])
     ts(tmp[:, 32:60], tmp[:, 0:28], 0.0, float(C), A.is_lt, A.mult, r=["t0"], w=["t1"])
@@ -231,13 +239,14 @@ def rank_program(g, core, T, topo):
     ts(k24[:, 48:72], tmp[:, 128:152], -64.0, 1.0, A.mult, A.add, r=["t4"], w=["cj"])
     cp(T.offg[:], tmp[:, 96:124], ["t3_"], ["offg"])
     pick("uc", "u", T.offc[:, 0:1], "offc")
-    post_u()
 
     iota(tmp[:, 192:384], [[0, 12], [1, 16]], 0, ["jm16"])
+    post_u()
     iota(k24[:, 72:96], [[0, 4], [64, 6]], 0, ["k64s"])
     iota(T.t2[:], [[1, 6], [6, 64]], 8, ["t2"])
     iota(T.t2[:, 63:C:64], [[1, 6]], 2, ["t2"])
     iota(T.t2[:, 318:C:64], [[1, 2]], 0, ["t2"])
+    iota(T.t3[:, 193:776], [[0, 583]], 0, ["t3b"])
     iota(T.nrow[:], [[1, 24], [24, 16]], 0, ["nrow"])
 
     def late_loads():
@@ -248,15 +257,12 @@ def rank_program(g, core, T, topo):
 
     def constants_b():
         ts(T.offr[:], pat[:, 104:110], cf, h16, A.add, A.add, r=["pa4", "pf"], w=["offr"])
-        ms(T.et[:, 512:2048], 0.0, ["et1", "et2", "et3"])
         ts(T.mum[:, 0:32], pat[:, 112:144], h16, None, A.is_equal, r=["pa5", "pf"], w=["mu_u"])
-        for b in range(4):
-            ts(T.et[:, 512 * b + b:512 * b + 512:4], T.t3[:, 0:128], pp, None, A.is_equal, r=["t3a", "pf"], w=["et%d" % b])
         ts(T.mum[:, 32:64], pat[:, 112:144], h16, BIG, A.not_equal, A.mult, r=["pa5", "pf"], w=["mu_t"])
-        quant("e", 0, 512, T.et[:], ["et0", "et1", "et2", "et3"])
         ts(T.mask4[:, 0:32], pat[:, 144:176], cf, -1.0, A.is_ge, A.mult, r=["pa6", "pf"], w=["m4a"])
         ts(T.mask4[:, 32:64], pat[:, 144:176], cf, None, A.is_lt, r=["pa6", "pf"], w=["m4b"])
         ts(k24[:, 96:144:2], pat[:, 176:200], c24, None, A.add, r=["pa7", "c24"], w=["n193"])
+        quant("e", 0, 512, T.et[:], ["et0", "et1", "et2", "et3"])
         ts(pf[:, 5:6], cf, 15.0, 1.0 / HI, A.is_equal, A.max, r=["pf"], w=["kap"])
         ts(pf[:, 6:7], cf, 1.0, None, A.add, r=["pf"], w=["c1"])
         ts(tmp[:, 0:24], k24[:, 24:48], -203.5, 1.0 / 24.0, A.add, A.mult, r=["base"], w=["t0"])
@@ -269,7 +275,6 @@ def rank_program(g, core, T, topo):
         tt(T.mud[:], T.dg[:], T.dg2[:, 0:192], A.add, r=["dg", "dg2a"], w=["mud"])
         cp(T.offp[:], tmp[:, 96:120], ["t3_"], ["offp"])
         pick("sl0", "lx0", T.cu[:, 24:32], "cu", s=slice(C, C + 16))
-        ms(T.t3[:, 193:776], 0.0, ["t3b"])
 
     def own_side(t):
         x = "x%d" % t
@@ -291,11 +296,11 @@ def rank_program(g, core, T, topo):
         ts(T.offa[:], sm[:, 56:80], sm[:, 1:2], None, A.subtract, r=["car3", "am"], w=["offa"])
         tr(T.ts[:], T.g1[:], ["g1"], ["ts"])
 
-    def argmin(i):
-        for k in range(6 * i, 6 * i + 6):
+    def argmin(k0, k1):
+        for k in range(k0, k1):
             op("a", lambda q: q.activation(T.aj[:, 64 * k:64 * k + 64], T.rr[:, 64 * k:64 * k + 64], ACT.Sign,
                                            bias=T.rr[:, 64 * k + 63:64 * k + 64], scale=-1.0, accum_out=T.jm[:, k:k + 1]),
-               ["rr%d" % i], ["aj%d" % k, "jm%d" % k])
+               ["rr%d" % (k // 6)], ["aj%d" % k, "jm%d" % k])
 
     def one_round(t):
         lx = "lx%d" % t
@@ -307,15 +312,16 @@ def rank_program(g, core, T, topo):
             for kk in range(k0, k1):
                 op("a", lambda q: q.activation(T.aa[:, 64 * kk:64 * kk + 64], bank(0, (kk + 2) % 6, C, 6), ACT.Abs,
                                                bias=T.ts[:, 16 * kk:16 * kk + 1], scale=-1.0), ["ts", "b0"], ["aa%d" % kk])
-            if i:
+            if i >= NI:
                 acp(T.ab[:, C * i:C * i + C], T.aa[:, C * i + 256:C * i + 640], ["aa%d" % kk for kk in range(6 * i + 4, 6 * i + 10)], ["ab%d" % i])
 
-        def larger(i):
+        def larger(i, k0=0, k1=6):
             a = C * i
-            if i == 0:
-                for k in range(6):
-                    tt(T.dd[:, 64 * k:64 * k + 64], T.aa[:, 0:64 * k + 256].indirect(T.offa[:, 4 * k:4 * k + 4]),
-                       T.aa[:, 64 * k + 256:64 * k + 320], A.max, ["aa%d" % kk for kk in range(k + 5)] + ["offa"], ["dd0_%d" % k])
+            if i < NI:
+                for k in range(k0, k1):
+                    tt(T.dd[:, a + 64 * k:a + 64 * k + 64], T.aa[:, a:a + 64 * k + 256].indirect(T.offa[:, 4 * k:4 * k + 4]),
+                       T.aa[:, a + 64 * k + 256:a + 64 * k + 320], A.max,
+                       ["aa%d" % kk for kk in range(6 * i, 6 * i + k + 5)] + ["offa"], ["dd%d_%d" % (i, k)])
             else:
                 tt(T.dd[:, a:a + C], T.aa[:, a:a + 576].indirect(T.offa[:]), T.ab[:, a:a + C], A.max,
                    ["aa%d" % kk for kk in range(6 * i, 6 * i + 9)] + ["offa", "ab%d" % i], ["dd%d_0" % i])
@@ -324,12 +330,11 @@ def rank_program(g, core, T, topo):
             a = C * i
             scan(T.rr[:, a:a + C], T.mumin[:], T.dd[:, a:a + C], 0.0, A.add, A.min, ["dd%d_%d" % (i, k) for k in range(6)] + ["mumin"], ["rr%d" % i])
 
-        def wide(i, f=acp, a=0, z=12, tag=""):
-            f(T.bb[:, 192 * i + 16 * a:192 * i + 16 * z], T.rr[:, C * i:C * i + C].indirect(T.cu[:, 32 + a:32 + z]),
-              ["rr%d" % i, "cu"], ["bb%d%s" % (i, tag)])
+        def wide(i, f=acp):
+            f(T.bb[:, 192 * i:192 * i + 192], T.rr[:, C * i:C * i + C].indirect(T.cu[:, 32:44]), ["rr%d" % i, "cu"], ["bb%d" % i])
 
         def turn(i):
-            tr(T.tt[:, 192 * i:192 * i + 192], T.bb[:, 192 * i:192 * i + 192], ["bb%d" % i, "bb%dv" % i], ["tt%d" % i])
+            tr(T.tt[:, 192 * i:192 * i + 192], T.bb[:, 192 * i:192 * i + 192], ["bb%d" % i], ["tt%d" % i])
 
         def rowp(i):
             acp(T.row[:, 96 * i:96 * i + 96], T.tt[:, 192 * i:192 * i + 192].indirect(T.offr[:]), ["tt%d" % i, "offr"], ["row%d" % i])
@@ -341,15 +346,12 @@ def rank_program(g, core, T, topo):
         rows, rrs = ["row%d" % i for i in range(4)], ["rr%d" % i for i in range(4)]
         mn, mx, lo, hi, m2 = (s3[:, 8 * i:8 * i + 8] for i in range(5))
         apart(0, 10, 0); apart(10, 16, 1); apart(16, 22, 2)
-        larger(0); least(0); larger(1)
-        wide(0); least(1); turn(0); apart(22, 28, 3); wide(1); rowp(0)
-        larger(2); turn(1); least(2)
-        argmin(0); wide(2); rowp(1); argmin(1)
-        larger(3)
+        larger(0); larger(1, 0, 1); least(0); larger(1, 1, 6); wide(0); apart(22, 28, 3)
+        larger(2); least(1); turn(0); least(2); wide(1); rowp(0); argmin(0, 6); wide(2)
+        larger(3); turn(1); least(3); rowp(1); argmin(6, 10)
         tt(mn, dm(0, 8), dm(8, 16), A.min, rrs[:3], ["mn"])
         tt(mx, dm(0, 8), dm(8, 16), A.max, rrs[:3], ["mx"])
-        turn(2); least(3)
-        rowp(2); wide(3, acp, 0, 6); wide(3, cp, 6, 12, "v")
+        wide(3, cp); turn(2); rowp(2)
         tt(m2, mx, dm(16, 24), A.min, ["mx"] + rrs, ["m2"])
         turn(3); rowp(3)
         cand, wv, dcol = s1[:, 0:16], s1[:, 16:32], s1[:, 32:56]
@@ -398,7 +400,7 @@ def rank_program(g, core, T, topo):
         for i in range(3, NA):
             count_a(1, i)
         total(1, 0); below(1, 2); total(1, 1); total(1, 2)
-        argmin(2); argmin(3)
+        argmin(10, 24)
         side_d(1); side_a(8, 8 + NA)
         cw = ["cand%d" % k for k in range(16)] + ["wv%d" % k for k in range(16)]
         tt(s1[:, 56:72], cand, wv, A.min, cw, ["du"])

from concourse.bass import DstId, RemoteDMATransfer
from concourse.mybir import dt, AluOpType, AxisListType, ActivationFunctionType

C, K, R = 384, 192, 3
STEP = [1, 3, 5]
BIG = 1.0e29
FAR = 2.0 ** 80
HI = 16384.0
NI = 2
NA, ND = 5, 3

F32, BF, I32, U16, Q8, U8 = "float32", "bfloat16", "int32", "uint16", "float8_e4m3fn_x4", "uint8"
SCRATCH = {"ps": ("psum", [128, 4096], F32)}
for _n, _w, _d in (
        [("xt%d" % t, 1536, BF) for t in range(4)] +
        [("ut", 512, BF), ("vt", 512, BF), ("zt", 768, BF), ("et", 2048, BF), ("mumin", 384, BF), ("ones", 384, BF),
         ("fl", 2 * ND * 384, BF), ("sc", 2 * ND * 384, BF), ("sj", 2 * NA * 384, BF), ("aj", 1536, BF), ("gt", 384, BF),
         ("ci", 64, I32), ("cu", 64, U16), ("pi", 8, I32), ("pf", 8, F32), ("pat", 256, F32), ("tmp", 512, F32),
         ("tmi", 32, I32), ("offc", 2, U16), ("offg", 28, U16), ("offr", 6, U16), ("offp", 24, U16),
         ("offa", 24, U16), ("offt", 4, U16), ("offd", 24, U16), ("offj", 24, U16), ("offz", 12, U16), ("offx", 24, U16),
         ("k24", 144, F32), ("mum", 64, F32), ("mask4", 64, F32), ("t3", 776, F32), ("t2", 384, F32),
         ("nrow", 384, F32), ("mud", 192, F32), ("mu75", 80, F32), ("mu64", 64, F32), ("eab", 128, F32),
         ("rsb", 768, F32), ("g1", 448, F32), ("ts", 448, F32), ("aa", 1792, F32), ("ab", 1536, F32), ("dd", 1536, F32),
         ("rr", 1536, F32), ("bb", 768, F32), ("tt", 768, F32), ("row", 384, F32), ("dc", 1536, F32), ("rs", 800, F32),
         ("win", 776, F32), ("win2", 776, F32), ("srow", 384, F32), ("row1", 384, F32), ("row2", 384, F32),
         ("dg", 192, F32), ("dg2", 384, F32), ("sm", 128, F32), ("sa", 32, F32), ("jm", 32, F32), ("s1", 128, F32),
         ("s3", 64, F32), ("mm", 64, F32), ("mt", 64, F32), ("ff", 80, F32), ("ll", 80, F32), ("gm", 64, F32),
         ("gs", 64, F32), ("yy", 80, F32), ("zz", 80, F32), ("ex", 80, F32), ("cm", 128, F32), ("yo", 384, F32)]):
    SCRATCH[_n] = ("sbuf", [128, _w], _d)
for _n, _w in ([("u", 128), ("uc", 16), ("so", 384), ("z", 192), ("e", 512), ("w", 512), ("v", 128)] +
               [("lu%d" % t, 16) for t in range(1, R)] + [("sl%d" % t, 128) for t in range(R)] +
               [("x%d" % t, 384 if t else 400) for t in range(R + 1)] + [("lx%d" % t, 384 if t else 400) for t in range(R)]):
    SCRATCH["q" + _n] = ("sbuf", [128, _w], Q8)
    SCRATCH["s" + _n + "p"] = ("sbuf", [128, _w], U8)

SEMAPHORES = ["cv", "ca", "cp", "cg", "sent", "arru", "arr0", "arr1", "arr2"] + ["d%d" % i for i in range(16)]

A = AluOpType
ACT = ActivationFunctionType


def rank_program(g, core, T, topo):
    rank = T.rank_of(core)
    if rank is None:
        return
    n_ranks = len(T.cores)
    Q = {"v": g.vector, "a": g.scalar, "p": g.tensor, "g": g, "s": g.sync}
    SEM = {"v": "cv", "a": "ca", "p": "cp", "g": "cg"}
    count = {}
    known = {e: {} for e in Q}
    wrote, reads = {}, {}
    ndma = [0]

    def need(e, ev):
        sem, val, clock = ev
        if known[e].get(sem, 0) < val:
            Q[e].wait_ge(T.sem[sem], val)
            known[e][sem] = val
            for s, x in clock.items():
                if known[e].get(s, 0) < x:
                    known[e][s] = x

    def op(e, call, r=(), w=(), sem=None, inc=1):
        evs = [wrote[k] for k in list(r) + list(w) if k in wrote]
        for k in w:
            evs += reads.get(k, [])
        for ev in sorted(evs, key=lambda x: -x[1]):
            need(e, ev)
        sem = sem or SEM[e]
        ins = call(Q[e])
        if ins is not None:
            ins.then_inc(T.sem[sem], inc)
        count[sem] = count.get(sem, 0) + inc
        ev = (sem, count[sem], dict(known[e]))
        for k in r:
            reads.setdefault(k, []).append(ev)
        for k in w:
            wrote[k] = ev
            reads[k] = []
        return ev

    def dma(e, out, in_, r=(), w=()):
        s = "d%d" % ndma[0]
        ndma[0] += 1
        op(e, lambda q: q.dma_start(out, in_), r, w, sem=s, inc=16)

    def ts(out, in0, s1, s2, o0, o1=None, r=(), w=()):
        if o1 is None:
            op("v", lambda q: q.tensor_scalar(out, in0, s1, None, o0), r, w)
        else:
            op("v", lambda q: q.tensor_scalar(out, in0, s1, s2, o0, o1), r, w)

    def tt(out, a, b, o, r=(), w=()):
        op("v", lambda q: q.tensor_tensor(out, a, b, o), r, w)

    def cp(out, in_, r=(), w=()):
        op("v", lambda q: q.tensor_copy(out, in_), r, w)

    def acp(out, in_, r=(), w=()):
        op("a", lambda q: q.activation(out, in_, ACT.Copy), r, w)

    def ms(ap, val, w):
        op("v", lambda q: q.memset(ap, val), (), w)

    def scan(out, d0, d1, init, o0, o1, r=(), w=()):
        op("v", lambda q: q.tensor_tensor_scan(out, d0, d1, init, o0, o1), r, w)

    def red(out, in_, o, r=(), w=()):
        op("v", lambda q: q.tensor_reduce(out, in_, AxisListType.X, o), r, w)

    def tr(out, in_, r=(), w=()):
        op("v", lambda q: q.transpose(out, in_), r, w)

    def iota(out, pat, base, w, cm=0, f=True):
        if f:
            op("g", lambda q: q.iota(out, pat, base, cm, allow_small_or_imprecise_dtypes=True), (), w)
        else:
            op("g", lambda q: q.iota(out, pat, base, cm), (), w)

    def quant(name, a, z, tile, r, tag=""):
        op("v", lambda q: q.quantize_mx(T["q" + name][:, a:z], T["s" + name + "p"][:, a:z], tile), r, ["q" + name + tag, "s" + name + tag])

    def mm(bank, st, a, mv, n):
        op("p", lambda q: q.matmul_mx(T.ps[:, 512 * bank:512 * bank + n], T["q" + st][:, a:a + 128], T["s" + st + "p"][:, a:a + 128],
                                      T["q" + mv][:, 0:n], T["s" + mv + "p"][:, 0:n], True, True),
           ["q" + st, "s" + st, "q" + mv, "s" + mv, "q" + mv + "h", "s" + mv + "h"], ["b%d" % bank])

    def pick(dst, src, off, key, d=slice(None), s=slice(None), tag=""):
        cp(T["q" + dst][:, d].bitcast(dt.uint32), T["q" + src][:, s].bitcast(dt.uint32).indirect(off), ["q" + src, key], ["q" + dst + tag])
        acp(T["s" + dst + "p"][:, d], T["s" + src + "p"][:, s].indirect(off), ["s" + src, key], ["s" + dst + tag])

    def bank(b, a=0, z=C, step=1):
        return T.ps[:, 512 * b + a:512 * b + z:step]

    askers = [T.cores[(rank - s) % n_ranks] for s in STEP]
    mask = topo.mask(core, askers[0])
    for c in askers:
        mask &= topo.mask(core, c)
    n_eng = bin(mask).count("1")

    def remote(call, r):
        op("g", call, r, (), sem="sent", inc=n_eng)

    def post(t, kind, cols, r):
        rid, pid = topo.addr(askers[t])[:2]
        arr = "arr%d" % t
        if kind == "q":
            dst, src = T["qlx%d" % t][:, cols].bitcast(dt.uint8), T["qx%d" % t][:, cols].bitcast(dt.uint8)
        else:
            dst, src = T["slx%dp" % t][:, cols], T["sx%dp" % t][:, cols]

        def call(q):
            q.remote_dma(dst, src, T.sem[arr], T.sem.sent, pid, rid, mask)
        remote(call, r)
        count[arr] = count.get(arr, 0) + n_eng
        wrote["qlx%d" % t] = wrote["slx%d" % t] = (arr, count[arr], {})

    def post_u():
        ids = [DstId(rid=topo.addr(c)[0], pnc=topo.addr(c)[1]) for c in askers[1:]]

        def codes(q):
            q.remote_dma_fused([RemoteDMATransfer(dst_ids=ids, dma_engine_mask=mask, remote_sem=T.sem.arru, srcs=[T.quc[:].bitcast(dt.uint8)],
                                                  dsts=[T["qlu%d" % t][:].bitcast(dt.uint8) for t in range(1, R)])], local_sem=T.sem.sent)

        def plane(q):
            q.remote_dma_fused([RemoteDMATransfer(dst_ids=ids, dma_engine_mask=mask, remote_sem=T.sem.arru, srcs=[T.sucp[:]],
                                                  dsts=[T["slu%dp" % t][:] for t in range(1, R)])], local_sem=T.sem.sent)
        remote(codes, ["quc"])
        remote(plane, ["suc"])
        count["arru"] = 2 * (R - 1) * n_eng
        for t in range(1, R):
            wrote["qlu%d" % t] = wrote["slu%d" % t] = ("arru", 2 * (R - 1) * n_eng, {})

    dma("s", T.ut[:], T.u[:], (), ["ut"])
    dma("a", T.xt0[:, 0:768], T.x[:, 0:768], (), ["x0a"])
    dma("s", T.xt0[:, 768:1536], T.x[:, 768:1536], (), ["x0b"])

    pat, pf, k24, tmp = T.pat, T.pf, T.k24, T.tmp
    iota(T.pi[:, 0:1], [[0, 1]], 0, ["pi0"], cm=1, f=False)
    iota(T.pi[:, 1:2], [[0, 1]], 0, ["pi1"], cm=16, f=False)
    iota(T.ci[:, 0:16], [[16, 2], [32, 4], [0, 2]], 0, ["ci0"], f=False)
    iota(T.ci[:, 16:24], [[16, 8]], 1, ["ci1"], f=False)
    iota(T.ci[:, 24:32], [[1, 8]], 0, ["ci2"], f=False)
    iota(T.ci[:, 32:44], [[64, 6], [0, 2]], 63, ["ci3"], f=False)
    iota(pat[:, 0:28], [[2, 14], [0, 2]], -4, ["pa0"])
    iota(pat[:, 28:56], [[0, 14], [C, 2]], 0, ["pa1"])
    iota(pat[:, 56:80], [[16, 24]], 0, ["pa2"])
    iota(pat[:, 80:104], [[0, 6], [16, 4]], 0, ["pa3"])
    iota(k24[:, 0:24], [[64, 6], [0, 4]], 0, ["s64"])
    iota(pat[:, 104:110], [[32, 6]], 0, ["pa4"])
    iota(pat[:, 112:144], [[16, 2], [0, 16]], 0, ["pa5"])
    iota(pat[:, 144:176], [[0, 2], [1, 16]], 0, ["pa6"])
    iota(pat[:, 176:200], [[1, 24]], 193, ["pa7"])

    ms(T.ones[:], 1.0, ["ones"])
    for i in range(6):
        a_, z_ = C * i, min(C * i + C, 2048)
        op("a", lambda q: q.activation(T.et[:, a_:z_], T.ones[:, 0:z_ - a_], ACT.Copy, scale=0.0), ["ones"], ["etz%d" % i])
    ms(T.mumin[:], 0.0, ["mumin"])
    ts(T.pi[:, 2:3], T.pi[:, 1:2], 127, None, A.bitwise_and, r=["pi1"], w=["pi2"])
    ts(T.pi[:, 4:5], T.pi[:, 0:1], 15, None, A.bitwise_and, r=["pi0"], w=["pi4"])
    ts(T.pi[:, 5:6], T.pi[:, 0:1], 16, None, A.bitwise_and, r=["pi0"], w=["pi5"])
    ts(T.pi[:, 6:7], T.pi[:, 0:1], 127, None, A.bitwise_and, r=["pi0"], w=["pi6"])
    ms(T.mu75[:], 1.0, ["mu75"])
    ms(pf[:, 7:8], 1.0, ["one"])
    ms(T.mu64[:], 1.0, ["mu64"])
    cp(T.offc[:, 0:1], T.pi[:, 2:3], ["pi2"], ["offc"])
    cp(pf[:, 0:3], T.pi[:, 4:7], ["pi4", "pi5", "pi6"], ["pf"])
    cf, h16, pp, c24 = pf[:, 0:1], pf[:, 1:2], pf[:, 2:3], pf[:, 3:4]
    scan(T.t3[:, 0:193], T.ones[:, 0:193], T.ones[:, 0:193], -1.0, A.mult, A.add, ["ones"], ["t3a"])
    ms(T.mumin[:, 0:C:64], BIG, ["mumin"])
    ms(T.ff[:], 0.0, ["ff0", "ff1", "ff2"])
    ms(T.rs[:, 0:800:200], 0.0, ["rs0"])
    ms(T.yy[:], 0.0, ["yya", "yyb"])
    ms(T.zz[:], 0.0, ["zza", "zzb"])
    ms(T.cm[:, 0:48], 0.0, ["out"])
    ms(T.mu75[:, 0:75:25], 0.0, ["mu75"])
    ms(T.mu64[:, 0:64:16], 0.0, ["mu64"])
    ts(pf[:, 3:4], cf, 24.0, None, A.mult, r=["pf"], w=["c24"])
    ts(pf[:, 4:5], h16, 0.0625, None, A.mult, r=["pf"], w=["hh"])
    cp(T.cu[:, 0:44], T.ci[:, 0:44], ["ci0", "ci1", "ci2", "ci3"], ["cu"])

    quant("u", 0, 128, T.ut[:], ["ut"])
    pick("x0", "u", T.offc[:, 0:1], "offc", d=slice(C, C + 16), tag="u")
    quant("x0", 0, C, T.xt0[:], ["x0a", "x0b"])
    post(0, "q", slice(None), ["qx0", "qx0u"])
    post(0, "s", slice(None), ["sx0", "sx0u"])
    op("a", lambda q: q.activation(T.eab[:], T.t3[:, 0:128], ACT.Abs, bias=pp, scale=-1.0), ["t3a", "pf"], ["eab"])
    pick("so", "u", T.cu[:, 0:24], "cu")
    for b in range(4):
        op("a", lambda q: q.activation(T.et[:, 512 * b + b:512 * b + 512:4], T.eab[:], ACT.Relu, bias=pf[:, 7:8], scale=-1.0),
           ["eab", "one"] + ["etz%d" % i for i in range(6)], ["et%d" % b])
    ts(tmp[:, 0:28], pat[:, 0:28], c24, pf[:, 4:5], A.add, A.add, r=["pa0", "c24", "hh"], w=["t0"])
    ts(k24[:, 24:48], pat[:, 56:80], cf, 192.0, A.add, A.add, r=["pa2", "pf"], w=["base"])
    ts(tmp[:, 32:60], tmp[:, 0:28], 0.0, float(C), A.is_lt, A.mult, r=["t0"], w=["t1"])
    tt(tmp[:, 64:92], tmp[:, 0:28], pat[:, 28:56], A.add, r=["t0", "pa1"], w=["t2_"])
    ts(tmp[:, 128:152], pat[:, 80:104], cf, 0.0, A.add, A.is_equal, r=["pa3", "pf"], w=["t4"])
    tt(tmp[:, 96:124], tmp[:, 64:92], tmp[:, 32:60], A.add, r=["t1", "t2_"], w=["t3_"])
    ts(k24[:, 48:72], tmp[:, 128:152], -64.0, 1.0, A.mult, A.add, r=["t4"], w=["cj"])
    cp(T.offg[:], tmp[:, 96:124], ["t3_"], ["offg"])
    pick("uc", "u", T.offc[:, 0:1], "offc")

    iota(tmp[:, 192:384], [[0, 12], [1, 16]], 0, ["jm16"])
    post_u()
    iota(k24[:, 72:96], [[0, 4], [64, 6]], 0, ["k64s"])
    iota(T.t2[:], [[1, 6], [6, 64]], 8, ["t2"])
    iota(T.t2[:, 63:C:64], [[1, 6]], 2, ["t2"])
    iota(T.t2[:, 318:C:64], [[1, 2]], 0, ["t2"])
    iota(T.t3[:, 193:776], [[0, 583]], 0, ["t3b"])
    iota(T.nrow[:], [[1, 24], [24, 16]], 0, ["nrow"])

    def late_loads():
        need("s", ("sent", count["sent"], {}))
        dma("s", T.qw[:].bitcast(dt.uint8), T.wc[:], (), ["qw"])
        dma("s", T.swp[:], T.ws[:], (), ["sw"])
        dma("s", T.vt[:], T.v[:], (), ["vt"])

    def constants_b():
        ts(T.offr[:], pat[:, 104:110], cf, h16, A.add, A.add, r=["pa4", "pf"], w=["offr"])
        ts(T.mum[:, 0:32], pat[:, 112:144], h16, None, A.is_equal, r=["pa5", "pf"], w=["mu_u"])
        ts(T.mum[:, 32:64], pat[:, 112:144], h16, BIG, A.not_equal, A.mult, r=["pa5", "pf"], w=["mu_t"])
        ts(T.mask4[:, 0:32], pat[:, 144:176], cf, -1.0, A.is_ge, A.mult, r=["pa6", "pf"], w=["m4a"])
        ts(T.mask4[:, 32:64], pat[:, 144:176], cf, None, A.is_lt, r=["pa6", "pf"], w=["m4b"])
        ts(k24[:, 96:144:2], pat[:, 176:200], c24, None, A.add, r=["pa7", "c24"], w=["n193"])
        quant("e", 0, 512, T.et[:], ["et0", "et1", "et2", "et3"])
        ts(pf[:, 5:6], cf, 15.0, 1.0 / HI, A.is_equal, A.max, r=["pf"], w=["kap"])
        ts(pf[:, 6:7], cf, 1.0, None, A.add, r=["pf"], w=["c1"])
        ts(tmp[:, 0:24], k24[:, 24:48], -203.5, 1.0 / 24.0, A.add, A.mult, r=["base"], w=["t0"])
        ts(tmp[:, 32:56], k24[:, 24:48], -192.0, 16.0, A.add, A.mult, r=["base"], w=["t1"])
        cp(T.tmi[:, 0:24], tmp[:, 0:24], ["t0"], ["tmi"])
        ts(T.dg[:], tmp[:, 192:384], cf, None, A.not_equal, r=["jm16", "pf"], w=["dg"])
        ts(tmp[:, 64:88], T.tmi[:, 0:24], -383.0, None, A.mult, r=["tmi"], w=["t2_"])
        ts(T.dg2[:, 0:192], tmp[:, 192:384], pf[:, 6:7], HI - 1.0, A.is_equal, A.mult, r=["jm16", "c1"], w=["dg2a"])
        tt(tmp[:, 96:120], tmp[:, 64:88], tmp[:, 32:56], A.add, r=["t1", "t2_"], w=["t3_"])
        tt(T.mud[:], T.dg[:], T.dg2[:, 0:192], A.add, r=["dg", "dg2a"], w=["mud"])
        cp(T.offp[:], tmp[:, 96:120], ["t3_"], ["offp"])
        pick("sl0", "lx0", T.cu[:, 24:32], "cu", s=slice(C, C + 16))

    def own_side(t):
        x = "x%d" % t
        mm(3, "so", 256, x, C)
        mm(1, "so", 0, x, C)
        mm(2, "so", 128, x, C)
        sm = T.sm
        ts(T.gt[:], bank(3), 0.0, None, A.is_gt, r=[], w=["gt", "b3"])
        acp(T.rsb[:, 0:C], bank(1), [], ["rsb0", "b1"])
        acp(T.rsb[:, C:2 * C], bank(2), [], ["rsb1", "b2"])
        acp(T.g1[:], T.rsb[:].indirect(T.offg[:]), ["rsb0", "rsb1", "offg"], ["g1"])
        red(sm[:, 0:1], T.gt[:], A.add, ["gt"], ["cnt"])
        ts(T.tmi[:, 24:25], sm[:, 0:1], 64.0, None, A.mult, r=["cnt"], w=["cnti"])
        ts(T.tmi[:, 26:27], T.tmi[:, 24:25], 192, None, A.bitwise_and, r=["cnti"], w=["ami"])
        cp(sm[:, 1:2], T.tmi[:, 26:27], ["ami"], ["am"])
        ts(sm[:, 8:32], k24[:, 0:24], sm[:, 1:2], None, A.is_le, r=["s64", "am"], w=["car"])
        tt(sm[:, 32:56], sm[:, 8:32], k24[:, 48:72], A.mult, ["car", "cj"], ["car2"])
        tt(sm[:, 56:80], k24[:, 24:48], sm[:, 32:56], A.subtract, ["car2", "base"], ["car3"])
        ts(T.offa[:], sm[:, 56:80], sm[:, 1:2], None, A.subtract, r=["car3", "am"], w=["offa"])
        tr(T.ts[:], T.g1[:], ["g1"], ["ts"])

    def argmin(k0, k1):
        for k in range(k0, k1):
            op("a", lambda q: q.activation(T.aj[:, 64 * k:64 * k + 64], T.rr[:, 64 * k:64 * k + 64], ACT.Sign,
                                           bias=T.rr[:, 64 * k + 63:64 * k + 64], scale=-1.0, accum_out=T.jm[:, k:k + 1]),
               ["rr%d" % (k // 6)], ["aj%d" % k, "jm%d" % k])

    def one_round(t):
        lx = "lx%d" % t
        mm(0, "sl%d" % t, 0, lx, C)
        for b in range(4):
            mm(4 + b, "e", 128 * b, lx, C)

        def apart(k0, k1, i):
            for kk in range(k0, k1):
                op("a", lambda q: q.activation(T.aa[:, 64 * kk:64 * kk + 64], bank(0, (kk + 2) % 6, C, 6), ACT.Abs,
                                               bias=T.ts[:, 16 * kk:16 * kk + 1], scale=-1.0), ["ts", "b0"], ["aa%d" % kk])
            if i >= NI:
                acp(T.ab[:, C * i:C * i + C], T.aa[:, C * i + 256:C * i + 640], ["aa%d" % kk for kk in range(6 * i + 4, 6 * i + 10)], ["ab%d" % i])

        def larger(i, k0=0, k1=6):
            a = C * i
            if i < NI:
                for k in range(k0, k1):
                    tt(T.dd[:, a + 64 * k:a + 64 * k + 64], T.aa[:, a:a + 64 * k + 256].indirect(T.offa[:, 4 * k:4 * k + 4]),
                       T.aa[:, a + 64 * k + 256:a + 64 * k + 320], A.max,
                       ["aa%d" % kk for kk in range(6 * i, 6 * i + k + 5)] + ["offa"], ["dd%d_%d" % (i, k)])
            else:
                tt(T.dd[:, a:a + C], T.aa[:, a:a + 576].indirect(T.offa[:]), T.ab[:, a:a + C], A.max,
                   ["aa%d" % kk for kk in range(6 * i, 6 * i + 9)] + ["offa", "ab%d" % i], ["dd%d_0" % i])

        def least(i):
            a = C * i
            scan(T.rr[:, a:a + C], T.mumin[:], T.dd[:, a:a + C], 0.0, A.add, A.min, ["dd%d_%d" % (i, k) for k in range(6)] + ["mumin"], ["rr%d" % i])

        def wide(i, f=acp):
            f(T.bb[:, 192 * i:192 * i + 192], T.rr[:, C * i:C * i + C].indirect(T.cu[:, 32:44]), ["rr%d" % i, "cu"], ["bb%d" % i])

        def turn(i):
            tr(T.tt[:, 192 * i:192 * i + 192], T.bb[:, 192 * i:192 * i + 192], ["bb%d" % i], ["tt%d" % i])

        def rowp(i):
            acp(T.row[:, 96 * i:96 * i + 96], T.tt[:, 192 * i:192 * i + 192].indirect(T.offr[:]), ["tt%d" % i, "offr"], ["row%d" % i])

        def dm(k0, k1):
            return T.rr[:, 64 * k0 + 63:64 * k1:64]

        s1, s3 = T.s1, T.s3
        rows, rrs = ["row%d" % i for i in range(4)], ["rr%d" % i for i in range(4)]
        mn, mx, lo, hi, m2 = (s3[:, 8 * i:8 * i + 8] for i in range(5))
        apart(0, 10, 0); apart(10, 16, 1); apart(16, 22, 2)
        larger(0); larger(1, 0, 1); least(0); larger(1, 1, 6); wide(0); apart(22, 28, 3)
        larger(2); least(1); turn(0); least(2); wide(1); rowp(0); argmin(0, 6); wide(2)
        larger(3); turn(1); least(3); rowp(1); argmin(6, 10)
        tt(mn, dm(0, 8), dm(8, 16), A.min, rrs[:3], ["mn"])
        tt(mx, dm(0, 8), dm(8, 16), A.max, rrs[:3], ["mx"])
        wide(3, cp); turn(2); rowp(2)
        tt(m2, mx, dm(16, 24), A.min, ["mx"] + rrs, ["m2"])
        turn(3); rowp(3)
        cand, wv, dcol = s1[:, 0:16], s1[:, 16:32], s1[:, 32:56]
        tt(s1[:, 0:8], mn, m2, A.max, ["mn", "m2"], ["cand%d" % i for i in range(8)])
        tt(lo, mn, dm(16, 24), A.min, ["mn"] + rrs, ["lo"])
        tt(hi, mx, dm(16, 24), A.max, ["mx"] + rrs, ["hi"])

        def count_a(p, i):
            j = NA * p + i
            op("a", lambda q: q.activation(T.sj[:, C * j:C * j + C], T.row[:], ACT.Sign, bias=s1[:, 8 * p + i:8 * p + i + 1], scale=-1.0,
                                           accum_out=T.sa[:, 8 * p + i:8 * p + i + 1]), rows + ["cand%d" % (8 * p + i)], ["sj%d" % j, "sa%d" % (8 * p + i)])

        def below(p, i):
            j, k = ND * p + i, 8 * p + NA + i
            ts(T.fl[:, C * j:C * j + C], T.row[:], s1[:, k:k + 1], -FAR, A.is_lt, A.mult, r=rows + ["cand%d" % k], w=["fl%d" % j])

        def total(p, i):
            j = ND * p + i
            scan(T.sc[:, C * j:C * j + C], T.ones[:], T.fl[:, C * j:C * j + C], (K - 0.5) * FAR, A.mult, A.add, ["fl%d" % j, "ones"], ["sc%d" % j])

        def side_a(k0, k1):
            ts(s1[:, 16 + k0:16 + k1], T.sa[:, k0:k1], -FAR, None, A.mult, r=["sa%d" % k for k in range(k0, k1)], w=["wv%d" % k for k in range(k0, k1)])

        def side_d(p):
            cp(s1[:, 16 + 8 * p + NA:24 + 8 * p], T.sc[:, C * ND * p + C - 1:C * ND * (p + 1):C], ["sc%d" % (ND * p + i) for i in range(ND)],
               ["wv%d" % (8 * p + NA + i) for i in range(ND)])

        def cap(k0, k1, w=None, r=None):
            tt(s3[:, 40 + k0:40 + k1], s3[:, 24 + k0:24 + k1], s1[:, 16 + k0:16 + k1] if w is None else w, A.min,
               ["hi"] + (r or ["wv%d" % k for k in range(k0, k1)]), ["cap%d" % k for k in range(k0, k1)])

        def next_one(k0, k1):
            tt(s1[:, 8 + k0:8 + k1], s3[:, 40 + k0:40 + k1], s3[:, 16 + k0:16 + k1], A.max,
               ["lo"] + ["cap%d" % k for k in range(k0, k1)], ["cand%d" % (8 + k) for k in range(k0, k1)])

        for i in range(NA):
            count_a(0, i)
        below(0, 0); below(0, 1); total(0, 0); below(0, 2); total(0, 1); side_a(0, 3); total(0, 2); cap(0, 3)
        cp(dcol, dm(0, 24), rrs, ["dcol"])
        next_one(0, 3)
        cap(NA, 8, T.sc[:, C - 1:C * ND:C], ["sc%d" % i for i in range(ND)])
        side_d(0); next_one(NA, 8)
        for i in range(3):
            count_a(1, i)
        side_a(3, NA); below(1, 0); cap(3, NA); below(1, 1); next_one(3, NA)
        for i in range(3, NA):
            count_a(1, i)
        total(1, 0); below(1, 2); total(1, 1); total(1, 2)
        argmin(10, 24)
        side_d(1); side_a(8, 8 + NA)
        cw = ["cand%d" % k for k in range(16)] + ["wv%d" % k for k in range(16)]
        tt(s1[:, 56:72], cand, wv, A.min, cw, ["du"])
        tt(s1[:, 72:88], cand, wv, A.max, cw, ["dt"])
        red(s1[:, 96:97], s1[:, 56:72], A.max, ["du"], ["up"])
        red(s1[:, 97:98], s1[:, 72:88], A.min, ["dt"], ["tp"])
        ts(T.mm[:, 0:32], T.mum[:, 0:32], s1[:, 96:97], None, A.mult, r=["mu_u", "up"], w=["mma"])
        ts(T.mm[:, 32:64], T.mum[:, 32:64], s1[:, 97:98], None, A.max, r=["mu_t", "tp"], w=["mmb"])
        tr(T.mt[:], T.mm[:], ["mma", "mmb"], ["mt"])
        red(s1[:, 98:99], T.mt[:, 0:32], A.max, ["mt"], ["uu"])
        red(s1[:, 99:100], T.mt[:, 32:64], A.min, ["mt"], ["tu"])
        ts(T.ff[:, 1:25], dcol, s1[:, 98:99], None, A.is_lt, r=["dcol", "uu"], w=["ff0"])
        ts(T.ff[:, 26:50], dcol, s1[:, 98:99], None, A.is_le, r=["dcol", "uu"], w=["ff1"])
        ts(T.ff[:, 51:75], dcol, s1[:, 99:100], None, A.is_le, r=["dcol", "tu"], w=["ff2"])
        for b in range(2):
            acp(T.dc[:, C * b:C * b + C], bank(4 + b), [], ["dc%d" % b, "b%d" % (4 + b)])
        scan(T.ll[:, 0:75], T.mu75[:, 0:75], T.ff[:, 0:75], 0.0, A.mult, A.add, ["ff0", "ff1", "ff2", "mu75"], ["ll"])
        cp(T.offt[:, 0:2], T.ll[:, 24:50:25], ["ll"], ["ofta"])
        cp(T.offt[:, 2:4], T.ll[:, 49:75:25], ["ll"], ["oftb"])
        tt(T.sm[:, 80:104], k24[:, 72:96], T.jm[:, 0:24], A.subtract, ["k64s"] + ["jm%d" % k for k in range(24)], ["jj"])
        tt(T.gm[:], T.t3[:, 0:32].indirect(T.offt[:]), T.mask4[:], A.mult, ["t3a", "ofta", "oftb", "m4a", "m4b"], ["gm"])
        cp(T.offj[:], T.sm[:, 80:104], ["jj"], ["offj"])
        acp(T.srow[:], T.t2[:].indirect(T.offj[:]), ["t2", "offj"], ["srow"])
        for b in range(2, 4):
            acp(T.dc[:, C * b:C * b + C], bank(4 + b), [], ["dc%d" % b, "b%d" % (4 + b)])
        scan(T.gs[:], T.mu64[:], T.gm[:], 0.0, A.mult, A.add, ["gm", "mu64"], ["gs"])
        ts(T.yy[:, 0:75:3], T.ll[:, 0:25], T.gs[:, 15:16], float(K), A.add, A.add, r=["ll", "gs"], w=["yya"])
        ts(T.zz[:, 1:75:3], T.ll[:, 25:50], T.gs[:, 47:48], None, A.add, r=["ll", "gs"], w=["zza"])
        ts(T.yy[:, 1:75:3], T.ll[:, 25:50], T.gs[:, 31:32], float(K), A.add, A.add, r=["ll", "gs"], w=["yyb"])
        ts(T.zz[:, 2:75:3], T.ll[:, 50:75], T.gs[:, 63:64], None, A.add, r=["ll", "gs"], w=["zzb"])
        scan(T.ex[:, 0:75], T.zz[:, 0:75], T.yy[:, 0:75], 0.0, A.min, A.max, ["yya", "yyb", "zza", "zzb"], ["cum"])
        cm = T.cm
        tt(cm[:, 1:48:2], T.ex[:, 2:74:3], T.ex[:, 5:75:3], A.is_equal, ["cum"], ["out"])
        cp(k24[:, 97:144:2], T.ex[:, 5:75:3], ["cum"], ["out2"])
        scan(cm[:, 64:112], cm[:, 0:48], k24[:, 96:144], 0.0, A.mult, A.add, ["out", "out2", "n193"], ["dst"])
        cp(T.offd[:], cm[:, 65:112:2], ["dst"], ["offd"])
        cp(T.win[:].indirect(T.offd[:]), T.srow[:], ["srow", "offd"], ["win"])
        acp(T.row1[:], T.t3[:].indirect(T.offd[:]), ["t3a", "t3b", "offd"], ["row1_"])
        acp(T.row2[:], T.row1[:].indirect(T.offp[:]), ["row1_", "offp"], ["row2_"])
        scan(T.dg[:], T.mud[:], T.win[:, 1:193], 0.0, A.mult, A.add, ["win", "mud"], ["dg"])
        ts(T.offz[:], T.dg[:, 15:192:16], pf[:, 5:6], None, A.mult, r=["dg", "kap"], w=["offz"])
        for b in range(4):
            (cp if b < 2 else acp)(T.zt[:, b:768:4], T.dc[:, C * b:C * b + C].indirect(T.offz[:]), ["dc%d" % b, "offz"], ["zt%d" % b])
        quant("z", 0, K, T.zt[:], ["zt%d" % b for b in range(4)])
        scan(T.dg2[:, 0:192], T.mud[:], T.row2[:, 0:192], 0.0, A.mult, A.add, ["row2_", "mud"], ["dg2a"])
        scan(T.dg2[:, 192:C], T.mud[:], T.row2[:, 192:C], 0.0, A.mult, A.add, ["row2_", "mud"], ["dg2b"])
        ts(T.offx[:, 0:12], T.dg2[:, 15:K:16], pf[:, 5:6], None, A.mult, r=["dg2a", "kap"], w=["offx0"])
        ts(T.offx[:, 12:24], T.dg2[:, K + 15:C:16], pf[:, 5:6], None, A.mult, r=["dg2b", "kap"], w=["offx1"])
        for b in range(4):
            mm(b, "w", 128 * b, "z", K)
            op("a", lambda q: q.activation(T.rs[:, 200 * b + 1:200 * b + 193], bank(b, 0, K), ACT.Copy, scale=0.015625),
               [], ["rs_%d" % b, "b%d" % b])
        old = ["x0a", "x0b"] if t == 0 else ["xt%d_%d" % (t, b) for b in range(8)]
        xo, xn, nx = T["xt%d" % t], T["xt%d" % (t + 1)], "x%d" % (t + 1)
        halves = [(0, 12), (12, 24)] if t + 1 < R else [(0, 24)]
        for h, (a, z) in enumerate(halves):
            keys = ["xt%d_%d" % (t + 1, 4 * h + b) for b in range(4)]
            for b in range(4):
                tt(xn[:, 64 * a + b:64 * z:4], T.rs[:, 200 * b:200 * b + 193].indirect(T.offx[:, a:z]), xo[:, 64 * a + b:64 * z:4], A.add,
                   ["rs0", "rs_%d" % b, "offx0"] + (["offx1"] if z > 12 else []) + old, [keys[b]])
            quant(nx, 16 * a, 16 * z, xn[:, 64 * a:64 * z], keys, tag="h" if h else "")
            if t + 1 < R:
                post(t + 1, "q", slice(16 * a, 16 * z), ["q" + nx + ("h" if h else "")])
        if t + 1 < R:
            post(t + 1, "s", slice(None), ["s" + nx, "s" + nx + "h"])

    late_loads()
    for t in range(R):
        own_side(t)
        if t == 0:
            constants_b()
        else:
            pick("sl%d" % t, "lu%d" % t, T.cu[:, 24:32], "cu")
        if t == 1:
            quant("v", 0, 128, T.vt[:], ["vt"])
        one_round(t)

    mm(4, "v", 0, "x3", C)
    dma("s", T.oc[:], T.qx3[:].bitcast(dt.uint8), ["qx3"], [])
    for k in range(4):
        dma("s", T.osc[4 * k:4 * k + 4, :], T.sx3p[32 * k:32 * k + 4, :], ["sx3"], [])
    acp(T.yo[:], bank(4), [], ["yo", "b4"])
    dma("a", T.y[:], T.yo[:], ["yo"], [])
    cp(T.win2[:].indirect(T.offd[:]), T.nrow[:], ["nrow", "offd"], ["win2"])
    dma("s", T.oe[:], T.win2[0:128:16, 1:193], ["win2"], [])
    for s in SEMAPHORES:
        if count.get(s, 0):
            need("g", (s, count[s], {}))
